import numpy as np
import ml_dtypes


def mxq(x, axis, fmt="e4m3"):
    dtype, down = {"e4m3": (ml_dtypes.float8_e4m3fn, 7), "e5m2": (ml_dtypes.float8_e5m2, 14)}[fmt]
    v = np.moveaxis(np.asarray(x, np.float32).astype(ml_dtypes.bfloat16).astype(np.float64), axis, -1)
    blocks = v.reshape(v.shape[:-1] + (-1, 32))
    amax = np.abs(blocks).max(-1, keepdims=True)
    byte = np.maximum(np.where(amax > 0, np.frexp(amax)[1] - 1 + 127, 0) - down, 1)
    scale = np.exp2(byte - 127.0)
    codes = (blocks / scale).astype(np.float32).astype(dtype).astype(np.float64)
    return np.moveaxis((codes * scale).reshape(v.shape), -1, axis)


WIDE = False


def mx_kscale(k):
    if not WIDE:
        return np.ones(k)
    levels = np.array([10, -10, 5, -5, 0])
    if k % 512:
        return np.exp2(np.random.permutation(np.resize(levels, k // 32))).repeat(32)
    a = np.empty((k // 512, 16))
    for p in range(k // 512):
        a[p, :8] = np.random.permutation(np.resize(levels, 8))
        for g in range(8):
            far = levels[np.abs(levels - a[p, g]) >= 10]
            a[p, g + 8] = far[np.random.randint(len(far))]
    return np.exp2(a.ravel()).repeat(32)


def f64(x):
    return np.asarray(x).astype(np.float64)


def striped(idx):
    return np.tile(idx.reshape(-1, 16).T, (8, 1)).astype(np.uint16)


def unstriped(offs):
    return offs[:16].T.reshape(-1).astype(np.int64)


E2M1 = np.array([0.0, 0.5, 1.0, 1.5, 2.0, 3.0, 4.0, 6.0, -0.0, -0.5, -1.0, -1.5, -2.0, -3.0, -4.0, -6.0])


def pack_weight(w, fmt):
    k, n = w.shape
    w = f64(np.asarray(w, np.float32).astype(ml_dtypes.bfloat16)).reshape(k // 32, 32, n)
    amax = np.abs(w).max(1)
    if fmt == "e4m3":
        byte = np.frexp(amax)[1] - 1 + 127 - 7
    else:
        mant, ex = np.frexp(amax / 6.0)
        byte = np.where(mant > 0.5, ex, ex - 1) + 127
    byte = np.clip(np.where(amax > 0, byte, 1), 1, 254)
    scaled = (w * np.exp2(127.0 - byte)[:, None, :]).reshape(k, n).astype(np.float32)
    by_word = np.ascontiguousarray(scaled.reshape(k // 512, 128, 4, n).transpose(0, 1, 3, 2))
    if fmt == "e4m3":
        words = by_word.astype(ml_dtypes.float8_e4m3fn).view(np.uint8)
    else:
        c = by_word.astype(ml_dtypes.float4_e2m1fn).view(np.uint8) & 0xF
        words = (c[..., 0::2] | (c[..., 1::2] << 4)).reshape(k // 512, 128, 2 * n)
    return np.ascontiguousarray(words), np.ascontiguousarray(byte.astype(np.uint8).reshape(k // 512, 16, n))


def unpack_weight(words, scales, fmt):
    g, _, n = scales.shape
    words = np.ascontiguousarray(words).reshape(g, 128, n, -1)
    if fmt == "e4m3":
        vals = words.view(ml_dtypes.float8_e4m3fn).astype(np.float64)
    else:
        nib = np.empty((g, 128, n, 4), np.uint8)
        nib[..., 0::2] = words & 0xF
        nib[..., 1::2] = words >> 4
        vals = E2M1[nib]
    vals = vals * np.repeat(np.exp2(scales.astype(np.float64) - 127.0), 8, axis=1)[..., None]
    return vals.transpose(0, 1, 3, 2).reshape(g * 512, n)


def gelu(v):
    return 0.5 * v * (1.0 + np.tanh(np.sqrt(2.0 / np.pi) * (v + 0.044715 * v**3)))


def pack_table4(v):
    words, scales = pack_weight(v, "e2m1")
    g, t = words.shape[0] // 2, v.shape[1]
    words = words.reshape(g, 2, 128, t, 2).transpose(0, 2, 3, 1, 4)
    return np.concatenate([words.reshape(g, -1), scales.reshape(g, -1)], axis=1)


def unpack_table4(tab):
    g, t = tab.shape[0], tab.shape[1] // 544
    words = tab[:, :512 * t].reshape(g, 128, t, 2, 2).transpose(0, 3, 1, 2, 4).reshape(2 * g, 128, 2 * t)
    return unpack_weight(words, tab[:, 512 * t:].reshape(2 * g, 16, t), "e2m1")


K, H, N, T, S = 2048, 512, 768, 2048, 1024

def setup_inputs():
    n = np.random.standard_normal
    s = mx_kscale(K)[:, None]
    u = mx_kscale(H)[:, None]
    tab = pack_table4(n((K, T)) * s)
    offs = striped(np.random.permutation(T)[:S])
    wd = (n((K, H)) / np.sqrt(K) / s * u.T).astype(np.float32)
    wc_words, wc_scales = pack_weight(n((K, H)) / np.sqrt(K) / s, "e2m1")
    wo_words, wo_scales = pack_weight(n((H, N)) / np.sqrt(H) / u, "e4m3")
    rate = np.exp(0.3 * n(N)).astype(np.float32)
    return {"tab": tab, "offs": offs, "wd": wd,
            "wc_words": wc_words, "wc_scales": wc_scales,
            "wo_words": wo_words, "wo_scales": wo_scales, "rate": rate}

def reference(tab, offs, wd, wc_words, wc_scales, wo_words, wo_scales, rate):
    v = unpack_table4(tab)[:, unstriped(offs)]
    wc = unpack_weight(wc_words, wc_scales, "e2m1")
    wo = unpack_weight(wo_words, wo_scales, "e4m3")
    d = mxq(f64(wd), 0, "e4m3").T @ v
    c = wc.T @ v
    h = d / np.sqrt(1.0 + np.square(c))
    y = wo.T @ mxq(h, 0, "e4m3")
    return f64(rate)[:, None] * y

@@ -1,0 +1,330 @@
+from contextlib import ExitStack
+
+import concourse.mybir as mybir
+
+K, H, N, T, S = 2048, 512, 768, 2048, 1024
+FLOPS = 2 * K * H * S * 2 + 2 * H * N * S
+
+F32 = mybir.dt.float32
+BF16 = mybir.dt.bfloat16
+I32 = mybir.dt.int32
+U32 = mybir.dt.uint32
+U16 = mybir.dt.uint16
+U8 = mybir.dt.uint8
+FP8X4 = mybir.dt.float8_e4m3fn_x4
+FP4X4 = mybir.dt.float4_e2m1fn_x4
+ACT = mybir.ActivationFunctionType
+MULT = mybir.AluOpType.mult
+
+P = 128
+PASSES = K // 512
+HALF = 512
+CHUNK = 128
+PAIR = 256
+NT = N // P
+WC0 = HALF
+WO0 = HALF + H
+ROW = HALF + H + N // 4
+
+
+def tile_list_momentum_block_steps_kernel(
+    tc, tab, offs, wd, wc_words, wc_scales, wo_words, wo_scales, rate, out
+):
+    nc = tc.nc
+    with ExitStack() as ctx:
+        keep = ctx.enter_context(tc.tile_pool(name="keep", bufs=1))
+        shared = ctx.enter_context(tc.tile_pool(name="shared", bufs=1))
+        ring = ctx.enter_context(tc.tile_pool(name="ring", bufs=2))
+        outp = ctx.enter_context(tc.tile_pool(name="outp", bufs=6))
+        psum = ctx.enter_context(tc.psum_pool(name="psum", bufs=8))
+
+        offsets = keep.tile([P, S // 16], U16, name="offsets")
+        tab_scale = keep.tile([P, T], U8, name="tab_scale", align_bytes=64)
+        tab_words = []
+        wc_raw = [keep.tile([P, 2, H], U16, name=f"wc_raw{m}", align_bytes=64) for m in range(2)]
+        wcs_raw = keep.tile([P, H], U8, name="wcs_raw", align_bytes=64)
+        stage = keep.tile([P, ROW], U8, name="stage", align_bytes=64)
+        wos = keep.tile([P, N], U8, name="wos", align_bytes=64)
+        planes = keep.tile([P, 4, ROW], U8, name="planes", align_bytes=64)
+        planes_b = keep.tile([P, 4, HALF], U8, name="planes_b", align_bytes=64)
+        warm = keep.tile([P, 2], F32, name="warm")
+
+        nc.vector.memset(warm[:, 0:1], 1.0)
+        nc.scalar.activation(warm[:, 1:2], warm[:, 0:1], ACT.Abs_reciprocal_sqrt, bias=1.0)
+        nc.vector.memset(wcs_raw[64:128, :].bitcast(I32), 0)
+        nc.vector.memset(tab_scale[64:128, :].bitcast(I32), 0)
+        nc.vector.memset(planes[:].rearrange("p a e -> p (a e)").bitcast(I32), 0)
+
+        nc.vector.memset(planes_b[:].rearrange("p a e -> p (a e)").bitcast(I32), 0)
+
+        def words(tile):
+            return tile.rearrange("p a e -> p (a e)").bitcast(I32).rearrange("p (a e) -> p a e", a=tile.shape[1])
+
+        for m in range(2):
+            nc.sync.dma_start(
+                tab_scale[m:64:2, :].bitcast(I32),
+                tab[m, 512 * T :].rearrange("(h q t) -> q h t", h=2, q=16).bitcast(I32),
+            )
+        nc.sync.dma_start(offsets[:], offs)
+        nc.scalar.dma_start(wcs_raw[0:64, :].bitcast(I32), wc_scales.bitcast(I32).rearrange("a q e -> q a e"))
+        nc.scalar.dma_start(
+            stage[0:64, WO0:ROW].bitcast(I32), wo_scales[0].rearrange("q (s e) -> (q s) e", s=4).bitcast(I32)
+        )
+
+        def load_wc(m):
+            nc.sync.dma_start(words(wc_raw[m][:]), wc_words.bitcast(I32)[2 * m : 2 * m + 2].rearrange("a p e -> p a e"))
+
+        def load_tab(m, tile):
+            tab_words.append(tile)
+            nc.sync.dma_start(
+                tab_words[m][:].bitcast(I32),
+                tab[m, 0 : 512 * T].rearrange("(p w) -> p w", p=P).bitcast(I32),
+            )
+
+        wd_raw = []
+
+        def load_wd(a, room):
+            raw = keep.tile([P, 4, H], F32, name=room, align_bytes=64)
+            nc.sync.dma_start(raw[:], wd[512 * a : 512 * (a + 1), :].rearrange("(p i) r -> p i r", i=4))
+            wd_raw.append(raw)
+
+        load_wc(0)
+        load_tab(0, keep.tile([P, T], U32, name="tab_words0", align_bytes=64))
+        load_wc(1)
+        wo_codes = keep.tile([P, N], U32, name="wo_codes", align_bytes=64)
+        nc.sync.dma_start(wo_codes[:].bitcast(I32), wo_words[0].rearrange("p e i -> p (e i)").bitcast(I32))
+
+        nc.vector.tensor_copy(
+            stage[:, WC0:WO0].rearrange("p (t c i) -> p c t i", t=4, i=16),
+            wcs_raw[:].rearrange("p (c i t) -> p c t i", t=4, i=16),
+        )
+        got_scale = shared.tile([P, HALF], U8, name="got_scale", align_bytes=64, offset=1792)
+        nc.vector.tensor_copy(got_scale[:], tab_scale[:].indirect(offsets[:, 0:32]))
+        nc.vector.tensor_copy(stage[0:64, 0:HALF].bitcast(I32), got_scale[0:64, :].bitcast(I32))
+        for q in range(4):
+            nc.sync.dma_start(words(planes[32 * q : 32 * q + 4]), stage[16 * q : 16 * q + 16, :].bitcast(I32))
+        load_tab(1, shared.tile([P, T], U32, name="tab_words1", align_bytes=64, offset=2048))
+
+        wc_codes = [
+            shared.tile([P, 2, H], U16, name="wc_codes0", align_bytes=64, offset=0),
+            shared.tile([P, 2, H], U16, name="wc_codes1", align_bytes=64, offset=10240),
+        ]
+
+        def order_wc(m):
+            nc.vector.tensor_copy(
+                wc_codes[m][:].rearrange("p a (t c i) -> p a c t i", t=4, i=8),
+                wc_raw[m][:].rearrange("p a (c i t) -> p a c t i", t=4, i=8),
+            )
+
+        v_codes = {}
+
+        def gather_words(m, b):
+            if (m, b) == (0, 0):
+                got = shared.tile([P, HALF], U32, name="got_first", align_bytes=64, offset=12032)
+            else:
+                got = shared.tile([P, HALF], U32, name="got", align_bytes=64, offset=12800)
+            nc.vector.tensor_copy(got[:], tab_words[m][:].indirect(offsets[:, 32 * b : 32 * (b + 1)]))
+            return got
+
+        def part_words(m, b, got):
+            codes = keep.tile([P, 2, HALF], U16, name=f"v_codes{m}{b}", align_bytes=64)
+            nc.vector.tensor_copy(
+                codes[:].rearrange("p h (c i) -> p c h i", i=8),
+                got[:].bitcast(U16).rearrange("p (c i h) -> p c h i", i=8, h=2),
+            )
+            v_codes[(m, b)] = codes
+
+        def v_operand(a, c0, width):
+            m, h = divmod(a, 2)
+            b, o = divmod(c0, HALF)
+            return (
+                v_codes[(m, b)][:, h, o : o + width].bitcast(FP4X4),
+                (planes, planes_b)[b][:, 2 * h + m, o : o + width],
+            )
+
+        wd_codes, wd_scale, wd_bf = [], [], []
+
+        def cast_wd(a, on_vector):
+            bf = keep.tile([P, 4, P, 4], BF16, name=f"wd_bf{a}", align_bytes=64)
+            dst = bf[:].rearrange("p t m i -> p m i t")
+            src = wd_raw[a][:].rearrange("p i (m t) -> p m i t", t=4)
+            if on_vector:
+                nc.vector.tensor_copy(dst, src)
+            else:
+                nc.scalar.copy(dst, src)
+            wd_bf.append(bf)
+
+        def quant_wd(a):
+            if a == 0:
+                codes = shared.tile([P, H], U32, name="got", align_bytes=64, offset=12800)
+            else:
+                codes = keep.tile([P, H], U32, name=f"wd_codes{a}", align_bytes=64)
+            scale = keep.tile([P, H], U8, name=f"wd_scale{a}", align_bytes=64)
+            nc.vector.quantize_mx(
+                out=codes[:].bitcast(FP8X4), scales=scale[:], in_=wd_bf[a][:].rearrange("p t m i -> p (t m i)")
+            )
+            wd_codes.append(codes)
+            wd_scale.append(scale)
+
+        c_acc = [[psum.tile([P, HALF], F32, name="acc") for t in range(4)] for b in range(2)]
+
+        def c_pass(a, b, t):
+            rhs, rhs_scale = v_operand(a, HALF * b, HALF)
+            nc.tensor.matmul_mx(
+                out=c_acc[b][t][:],
+                lhsT=wc_codes[a // 2][:, a % 2, P * t : P * (t + 1)].bitcast(FP4X4),
+                lhsT_scale=planes[:, a, WC0 + P * t : WC0 + P * (t + 1)],
+                rhs=rhs,
+                rhs_scale=rhs_scale,
+                start=(a == 0),
+                stop=(a == PASSES - 1),
+            )
+
+        order_wc(0)
+        load_wd(0, "wc_raw0")
+        g00 = gather_words(0, 0)
+        part_words(0, 0, g00)
+        got_scale_b = shared.tile([P, HALF], U8, name="got_scale_b", align_bytes=64, offset=12288)
+        nc.vector.tensor_copy(got_scale_b[:], tab_scale[:].indirect(offsets[:, 32:64]))
+        for q in range(4):
+            nc.sync.dma_start(words(planes_b[32 * q : 32 * q + 4]), got_scale_b[16 * q : 16 * q + 16, :].bitcast(I32))
+        load_wd(1, "tab_scale")
+        order_wc(1)
+        load_wd(2, "wc_raw1")
+        for a in range(2):
+            for t in range(4):
+                c_pass(a, 0, t)
+        part_words(1, 0, gather_words(1, 0))
+        cast_wd(0, False)
+        load_wd(3, "wc_raw0")
+        for t in range(4):
+            c_pass(2, 0, t)
+            c_pass(3, 0, t)
+        part_words(0, 1, gather_words(0, 1))
+        for a in range(2):
+            for t in range(4):
+                c_pass(a, 1, t)
+        part_words(1, 1, gather_words(1, 1))
+        cast_wd(1, False)
+        for t in range(4):
+            c_pass(2, 1, t)
+            c_pass(3, 1, t)
+        quant_wd(0)
+
+        sq = [keep.tile([P, 4, HALF], F32, name=room, align_bytes=64) for room in ("tab_scale", "sq1")]
+        damp = [keep.tile([P, CHUNK, 4], F32, name=f"damp{i}") for i in range(S // CHUNK)]
+
+        def square(b, t):
+            nc.scalar.activation(sq[b][:, t, :], c_acc[b][t][:], ACT.Square)
+
+        def rsqrt(i):
+            b, o = divmod(CHUNK * i, HALF)
+            nc.scalar.activation(
+                damp[i][:].rearrange("p (c e) t -> p c t e", e=4),
+                sq[b][:, :, o : o + CHUNK].rearrange("p t (c e) -> p c t e", e=4),
+                ACT.Abs_reciprocal_sqrt,
+                bias=1.0,
+            )
+
+        for t in range(4):
+            square(0, t)
+        cast_wd(2, True)
+        quant_wd(1)
+        rate_sb = keep.tile([P, NT], F32, name="wc_raw1", align_bytes=64)
+        with nc.allow_non_contiguous_dma(reason="one rate for each output row"):
+            nc.sync.dma_start(rate_sb[:], rate.rearrange("(u p) -> p u", p=P))
+        quant_wd(2)
+        cast_wd(3, True)
+        for i in range(2):
+            rsqrt(i)
+        for t in range(4):
+            square(1, t)
+        for i in range(2, 4):
+            rsqrt(i)
+        quant_wd(3)
+        nc.vector.tensor_copy(
+            wos[:].bitcast(I32).rearrange("p (s e) -> p s e", s=4),
+            words(planes[:])[:, :, WO0 // 4 :],
+        )
+
+        d_acc = {}
+
+        def d_pass(a, i):
+            if a == 0:
+                d_acc[i] = psum.tile([P, 4, CHUNK], F32, name="acc")
+            rhs, rhs_scale = v_operand(a, CHUNK * i, CHUNK)
+            for t in range(4):
+                nc.tensor.matmul_mx(
+                    out=d_acc[i][:, t, :],
+                    lhsT=wd_codes[a][:, P * t : P * (t + 1)].bitcast(FP8X4),
+                    lhsT_scale=wd_scale[a][:, P * t : P * (t + 1)],
+                    rhs=rhs,
+                    rhs_scale=rhs_scale,
+                    start=(a == 0 and t == 0),
+                    stop=(a == PASSES - 1 and t == 3),
+                )
+
+        h_bf, h_codes, h_scale = {}, {}, {}
+
+        def damp_chunk(i):
+            g = i // 2
+            if i % 2 == 0:
+                h_bf[g] = ring.tile([P, 2, CHUNK, 4], BF16, name="h_bf", align_bytes=64)
+            nc.vector.tensor_tensor(
+                h_bf[g][:, i % 2], d_acc[i][:].rearrange("p t n -> p n t"), damp[i][:], MULT
+            )
+
+        def quant_h(g):
+            h_codes[g] = ring.tile([P, PAIR], U32, name="h_codes", align_bytes=64)
+            h_scale[g] = ring.tile([P, PAIR], U8, name="h_scale", align_bytes=64)
+            nc.vector.quantize_mx(
+                out=h_codes[g][:].bitcast(FP8X4),
+                scales=h_scale[g][:],
+                in_=h_bf[g][:].rearrange("p c n t -> p (c n t)"),
+            )
+
+        def step_out(g):
+            for bk in range(NT // 2):
+                acc = psum.tile([P, 2, PAIR], F32, name="acc")
+                for e in range(2):
+                    u = 2 * bk + e
+                    nc.tensor.matmul_mx(
+                        out=acc[:, e, :],
+                        lhsT=wo_codes[:, P * u : P * (u + 1)].bitcast(FP8X4),
+                        lhsT_scale=wos[:, P * u : P * (u + 1)],
+                        rhs=h_codes[g][:].bitcast(FP8X4),
+                        rhs_scale=h_scale[g][:],
+                        start=True,
+                        stop=True,
+                    )
+                res = outp.tile([P, 2, PAIR], F32, name="res")
+                for e in range(2):
+                    u = 2 * bk + e
+                    if bk == 1:
+                        nc.vector.tensor_scalar(res[:, e, :], acc[:, e, :], rate_sb[:, u : u + 1], None, MULT)
+                    else:
+                        nc.scalar.activation(res[:, e, :], acc[:, e, :], ACT.Copy, scale=rate_sb[:, u : u + 1])
+                nc.sync.dma_start(
+                    out[2 * P * bk : 2 * P * (bk + 1), PAIR * g : PAIR * (g + 1)].rearrange("(e p) j -> p e j", p=P),
+                    res[:],
+                )
+
+        for a in range(PASSES - 1):
+            for i in range(4):
+                d_pass(a, i)
+        for i in range(4):
+            d_pass(PASSES - 1, i)
+            damp_chunk(i)
+            if i % 2 == 1:
+                quant_h(i // 2)
+        for i in range(4, 8):
+            rsqrt(i)
+        for i in range(4, 8):
+            for a in range(PASSES):
+                d_pass(a, i)
+            damp_chunk(i)
+            if i % 2 == 1:
+                quant_h(i // 2)
+            if i < 7:
+                step_out(i - 4) if i < 6 else step_out(2)
+        step_out(3)

@@ -23,8 +23,7 @@ CHUNK = 128
 PAIR = 256
 NT = N // P
 WC0 = HALF
-WO0 = HALF + H
-ROW = HALF + H + N // 4
+ROW = HALF + H
 
 
 def tile_list_momentum_block_steps_kernel(
@@ -44,7 +43,6 @@ def tile_list_momentum_block_steps_kernel(
         wc_raw = [keep.tile([P, 2, H], U16, name=f"wc_raw{m}", align_bytes=64) for m in range(2)]
         wcs_raw = keep.tile([P, H], U8, name="wcs_raw", align_bytes=64)
         stage = keep.tile([P, ROW], U8, name="stage", align_bytes=64)
-        wos = keep.tile([P, N], U8, name="wos", align_bytes=64)
         planes = keep.tile([P, 4, ROW], U8, name="planes", align_bytes=64)
         planes_b = keep.tile([P, 4, HALF], U8, name="planes_b", align_bytes=64)
         warm = keep.tile([P, 2], F32, name="warm")
@@ -67,9 +65,6 @@ def tile_list_momentum_block_steps_kernel(
             )
         nc.sync.dma_start(offsets[:], offs)
         nc.scalar.dma_start(wcs_raw[0:64, :].bitcast(I32), wc_scales.bitcast(I32).rearrange("a q e -> q a e"))
-        nc.scalar.dma_start(
-            stage[0:64, WO0:ROW].bitcast(I32), wo_scales[0].rearrange("q (s e) -> (q s) e", s=4).bitcast(I32)
-        )
 
         def load_wc(m):
             nc.sync.dma_start(words(wc_raw[m][:]), wc_words.bitcast(I32)[2 * m : 2 * m + 2].rearrange("a p e -> p a e"))
@@ -95,14 +90,16 @@ def tile_list_momentum_block_steps_kernel(
         nc.sync.dma_start(wo_codes[:].bitcast(I32), wo_words[0].rearrange("p e i -> p (e i)").bitcast(I32))
 
         nc.vector.tensor_copy(
-            stage[:, WC0:WO0].rearrange("p (t c i) -> p c t i", t=4, i=16),
+            stage[:, WC0:ROW].rearrange("p (t c i) -> p c t i", t=4, i=16),
             wcs_raw[:].rearrange("p (c i t) -> p c t i", t=4, i=16),
         )
         got_scale = shared.tile([P, HALF], U8, name="got_scale", align_bytes=64, offset=1792)
         nc.vector.tensor_copy(got_scale[:], tab_scale[:].indirect(offsets[:, 0:32]))
         nc.vector.tensor_copy(stage[0:64, 0:HALF].bitcast(I32), got_scale[0:64, :].bitcast(I32))
         for q in range(4):
-            nc.sync.dma_start(words(planes[32 * q : 32 * q + 4]), stage[16 * q : 16 * q + 16, :].bitcast(I32))
+            (nc.sync, nc.scalar)[q // 2].dma_start(
+                words(planes[32 * q : 32 * q + 4]), stage[16 * q : 16 * q + 16, :].bitcast(I32)
+            )
         load_tab(1, shared.tile([P, T], U32, name="tab_words1", align_bytes=64, offset=2048))
 
         wc_codes = [
@@ -187,7 +184,9 @@ def tile_list_momentum_block_steps_kernel(
         got_scale_b = shared.tile([P, HALF], U8, name="got_scale_b", align_bytes=64, offset=12288)
         nc.vector.tensor_copy(got_scale_b[:], tab_scale[:].indirect(offsets[:, 32:64]))
         for q in range(4):
-            nc.sync.dma_start(words(planes_b[32 * q : 32 * q + 4]), got_scale_b[16 * q : 16 * q + 16, :].bitcast(I32))
+            (nc.sync, nc.scalar)[q // 2].dma_start(
+                words(planes_b[32 * q : 32 * q + 4]), got_scale_b[16 * q : 16 * q + 16, :].bitcast(I32)
+            )
         load_wd(1, "tab_scale")
         order_wc(1)
         load_wd(2, "wc_raw1")
@@ -230,6 +229,10 @@ def tile_list_momentum_block_steps_kernel(
             square(0, t)
         cast_wd(2, True)
         quant_wd(1)
+        wos = keep.tile([P, N], U8, name="tab_words0", align_bytes=64)
+        nc.gpsimd.memset(wos[:].bitcast(I32), 0)
+        for r in range(4):
+            nc.sync.dma_start(wos[r:P:32, :].bitcast(I32), wo_scales[0, r:16:4, :].bitcast(I32))
         rate_sb = keep.tile([P, NT], F32, name="wc_raw1", align_bytes=64)
         with nc.allow_non_contiguous_dma(reason="one rate for each output row"):
             nc.sync.dma_start(rate_sb[:], rate.rearrange("(u p) -> p u", p=P))
@@ -242,10 +245,6 @@ def tile_list_momentum_block_steps_kernel(
         for i in range(2, 4):
             rsqrt(i)
         quant_wd(3)
-        nc.vector.tensor_copy(
-            wos[:].bitcast(I32).rearrange("p (s e) -> p s e", s=4),
-            words(planes[:])[:, :, WO0 // 4 :],
-        )
 
         d_acc = {}
 

@@ -22,7 +22,6 @@ HALF = 512
 CHUNK = 128
 PAIR = 256
 NT = N // P
-WC0 = HALF
 ROW = HALF + H
 
 
@@ -33,224 +32,203 @@ def tile_list_momentum_block_steps_kernel(
     with ExitStack() as ctx:
         keep = ctx.enter_context(tc.tile_pool(name="keep", bufs=1))
         shared = ctx.enter_context(tc.tile_pool(name="shared", bufs=1))
-        ring = ctx.enter_context(tc.tile_pool(name="ring", bufs=2))
-        outp = ctx.enter_context(tc.tile_pool(name="outp", bufs=6))
-        psum = ctx.enter_context(tc.psum_pool(name="psum", bufs=8))
+        psum = ctx.enter_context(tc.psum_pool(name="psum", bufs=1))
 
-        offsets = keep.tile([P, S // 16], U16, name="offsets")
-        tab_scale = keep.tile([P, T], U8, name="tab_scale", align_bytes=64)
-        tab_words = []
-        wc_raw = [keep.tile([P, 2, H], U16, name=f"wc_raw{m}", align_bytes=64) for m in range(2)]
-        wcs_raw = keep.tile([P, H], U8, name="wcs_raw", align_bytes=64)
-        stage = keep.tile([P, ROW], U8, name="stage", align_bytes=64)
-        planes = keep.tile([P, 4, ROW], U8, name="planes", align_bytes=64)
-        planes_b = keep.tile([P, 4, HALF], U8, name="planes_b", align_bytes=64)
-        warm = keep.tile([P, 2], F32, name="warm")
+        def placed(shape, dtype, name, offset):
+            return shared.tile(shape, dtype, name=name, align_bytes=64, offset=offset)
 
-        nc.vector.memset(warm[:, 0:1], 1.0)
-        nc.scalar.activation(warm[:, 1:2], warm[:, 0:1], ACT.Abs_reciprocal_sqrt, bias=1.0)
-        nc.vector.memset(wcs_raw[64:128, :].bitcast(I32), 0)
-        nc.vector.memset(tab_scale[64:128, :].bitcast(I32), 0)
-        nc.vector.memset(planes[:].rearrange("p a e -> p (a e)").bitcast(I32), 0)
+        def kept(shape, dtype, name):
+            return keep.tile(shape, dtype, name=name, align_bytes=64)
 
-        nc.vector.memset(planes_b[:].rearrange("p a e -> p (a e)").bitcast(I32), 0)
+        def bank(shape, b):
+            return psum.tile(shape, F32, name=f"bank{b}")
 
         def words(tile):
             return tile.rearrange("p a e -> p (a e)").bitcast(I32).rearrange("p (a e) -> p a e", a=tile.shape[1])
 
+        offsets = keep.tile([P, S // 16], U16, name="offsets")
+        tab_scale = placed([P, T], U8, "tab_scale", 15360)
+        wcs_raw = kept([P, H], U8, "wcs_raw")
+        wc_raw = [kept([P, 2, H], U16, f"wc_raw{m}") for m in range(2)]
+        planes = [kept([P, 4, ROW], U8, "planes_a"), kept([P, 4, HALF], U8, "planes_b")]
+        warm = keep.tile([P, 2], F32, name="warm")
+
+        nc.vector.memset(warm[:, 0:1], 1.0)
+        nc.scalar.activation(warm[:, 1:2], warm[:, 0:1], ACT.Abs_reciprocal_sqrt, bias=1.0)
+        nc.vector.memset(tab_scale[64:128, :].bitcast(I32), 0)
+        nc.vector.memset(wcs_raw[64:128, :].bitcast(I32), 0)
+        for b in range(2):
+            nc.vector.memset(planes[b][:].rearrange("p a e -> p (a e)").bitcast(I32), 0)
+
+        nc.sync.dma_start(offsets[:], offs)
         for m in range(2):
             nc.sync.dma_start(
                 tab_scale[m:64:2, :].bitcast(I32),
                 tab[m, 512 * T :].rearrange("(h q t) -> q h t", h=2, q=16).bitcast(I32),
             )
-        nc.sync.dma_start(offsets[:], offs)
         nc.scalar.dma_start(wcs_raw[0:64, :].bitcast(I32), wc_scales.bitcast(I32).rearrange("a q e -> q a e"))
 
         def load_wc(m):
             nc.sync.dma_start(words(wc_raw[m][:]), wc_words.bitcast(I32)[2 * m : 2 * m + 2].rearrange("a p e -> p a e"))
 
         def load_tab(m, tile):
-            tab_words.append(tile)
-            nc.sync.dma_start(
-                tab_words[m][:].bitcast(I32),
-                tab[m, 0 : 512 * T].rearrange("(p w) -> p w", p=P).bitcast(I32),
-            )
+            nc.sync.dma_start(tile[:].bitcast(I32), tab[m, 0 : 512 * T].rearrange("(p w) -> p w", p=P).bitcast(I32))
+            return tile
 
-        wd_raw = []
-
-        def load_wd(a, room):
-            raw = keep.tile([P, 4, H], F32, name=room, align_bytes=64)
-            nc.sync.dma_start(raw[:], wd[512 * a : 512 * (a + 1), :].rearrange("(p i) r -> p i r", i=4))
-            wd_raw.append(raw)
+        def load_wd(a, raw, r0):
+            rows = wd[512 * a : 512 * (a + 1), r0 : r0 + raw.shape[2]]
+            nc.sync.dma_start(raw[:], rows.rearrange("(p i) r -> p i r", i=4))
+            return raw
 
         load_wc(0)
-        load_tab(0, keep.tile([P, T], U32, name="tab_words0", align_bytes=64))
+        tab_words = [load_tab(0, kept([P, T], U32, "tab_words0"))]
         load_wc(1)
-        wo_codes = keep.tile([P, N], U32, name="wo_codes", align_bytes=64)
-        nc.sync.dma_start(wo_codes[:].bitcast(I32), wo_words[0].rearrange("p e i -> p (e i)").bitcast(I32))
+        wd0_raw = [load_wd(0, kept([P, 4, H // 2], F32, "wd0_raw0"), 0)]
 
+        got_a = placed([P, HALF], U8, "got_a", 3072)
+        nc.vector.tensor_copy(got_a[:], tab_scale[:].indirect(offsets[:, 0:32]))
+        stage = placed([P, ROW], U8, "stage", 32256)
         nc.vector.tensor_copy(
-            stage[:, WC0:ROW].rearrange("p (t c i) -> p c t i", t=4, i=16),
+            stage[:, HALF:ROW].rearrange("p (t c i) -> p c t i", t=4, i=16),
             wcs_raw[:].rearrange("p (c i t) -> p c t i", t=4, i=16),
         )
-        got_scale = shared.tile([P, HALF], U8, name="got_scale", align_bytes=64, offset=1792)
-        nc.vector.tensor_copy(got_scale[:], tab_scale[:].indirect(offsets[:, 0:32]))
-        nc.vector.tensor_copy(stage[0:64, 0:HALF].bitcast(I32), got_scale[0:64, :].bitcast(I32))
+        nc.vector.tensor_copy(stage[0:64, 0:HALF].bitcast(I32), got_a[0:64, :].bitcast(I32))
         for q in range(4):
             (nc.sync, nc.scalar)[q // 2].dma_start(
-                words(planes[32 * q : 32 * q + 4]), stage[16 * q : 16 * q + 16, :].bitcast(I32)
+                words(planes[0][32 * q : 32 * q + 4]), stage[16 * q : 16 * q + 16, :].bitcast(I32)
             )
-        load_tab(1, shared.tile([P, T], U32, name="tab_words1", align_bytes=64, offset=2048))
+        tab_words.append(load_tab(1, placed([P, T], U32, "tab_words1", 3328)))
+        got_b = placed([P, HALF], U8, "got_b", 2816)
+        nc.vector.tensor_copy(got_b[:], tab_scale[:].indirect(offsets[:, 32:64]))
+        for q in (0, 2, 1, 3):
+            nc.scalar.dma_start(words(planes[1][32 * q : 32 * q + 4]), got_b[16 * q : 16 * q + 16, :].bitcast(I32))
+        wd0_raw.append(load_wd(0, placed([P, 4, H // 2], F32, "wd0_raw1", 11520), H // 2))
+        wd_raw = {
+            1: load_wd(1, placed([P, 4, H], F32, "wd_raw1", 16384), 0),
+            2: load_wd(2, placed([P, 4, H], F32, "wd_raw2", 24576), 0),
+            3: load_wd(3, placed([P, 4, H], F32, "wd_raw3", 32768), 0),
+        }
+        wo_codes = placed([P, N], U32, "wo_codes", 0)
+        nc.sync.dma_start(wo_codes[:].bitcast(I32), wo_words[0].rearrange("p e i -> p (e i)").bitcast(I32))
 
-        wc_codes = [
-            shared.tile([P, 2, H], U16, name="wc_codes0", align_bytes=64, offset=0),
-            shared.tile([P, 2, H], U16, name="wc_codes1", align_bytes=64, offset=10240),
-        ]
+        wc_codes, got, v_codes = {}, {}, {}
 
-        def order_wc(m):
+        def order_wc(m, codes):
+            wc_codes[m] = codes
             nc.vector.tensor_copy(
-                wc_codes[m][:].rearrange("p a (t c i) -> p a c t i", t=4, i=8),
+                codes[:].rearrange("p a (t c i) -> p a c t i", t=4, i=8),
                 wc_raw[m][:].rearrange("p a (c i t) -> p a c t i", t=4, i=8),
             )
 
-        v_codes = {}
+        def gather_words(m, b, tile):
+            got[(m, b)] = tile
+            nc.vector.tensor_copy(tile[:], tab_words[m][:].indirect(offsets[:, 32 * b : 32 * (b + 1)]))
 
-        def gather_words(m, b):
-            if (m, b) == (0, 0):
-                got = shared.tile([P, HALF], U32, name="got_first", align_bytes=64, offset=12032)
-            else:
-                got = shared.tile([P, HALF], U32, name="got", align_bytes=64, offset=12800)
-            nc.vector.tensor_copy(got[:], tab_words[m][:].indirect(offsets[:, 32 * b : 32 * (b + 1)]))
-            return got
-
-        def part_words(m, b, got):
-            codes = keep.tile([P, 2, HALF], U16, name=f"v_codes{m}{b}", align_bytes=64)
+        def part_words(m, b):
+            codes = kept([P, 2, HALF], U16, f"v_codes{m}{b}")
             nc.vector.tensor_copy(
                 codes[:].rearrange("p h (c i) -> p c h i", i=8),
-                got[:].bitcast(U16).rearrange("p (c i h) -> p c h i", i=8, h=2),
+                got[(m, b)][:].bitcast(U16).rearrange("p (c i h) -> p c h i", i=8, h=2),
             )
             v_codes[(m, b)] = codes
 
         def v_operand(a, c0, width):
             m, h = divmod(a, 2)
             b, o = divmod(c0, HALF)
-            return (
-                v_codes[(m, b)][:, h, o : o + width].bitcast(FP4X4),
-                (planes, planes_b)[b][:, 2 * h + m, o : o + width],
-            )
+            return v_codes[(m, b)][:, h, o : o + width].bitcast(FP4X4), planes[b][:, 2 * h + m, o : o + width]
 
-        wd_codes, wd_scale, wd_bf = [], [], []
+        wd_bf = [kept([P, 4, P, 4], BF16, f"wd_bf{a}") for a in range(PASSES)]
+        wd_codes, wd_scale = {}, {}
 
-        def cast_wd(a, on_vector):
-            bf = keep.tile([P, 4, P, 4], BF16, name=f"wd_bf{a}", align_bytes=64)
-            dst = bf[:].rearrange("p t m i -> p m i t")
-            src = wd_raw[a][:].rearrange("p i (m t) -> p m i t", t=4)
-            if on_vector:
-                nc.vector.tensor_copy(dst, src)
-            else:
-                nc.scalar.copy(dst, src)
-            wd_bf.append(bf)
+        def cast_wd(a, raw, m0, copy):
+            src = raw[:].rearrange("p i (m t) -> p m i t", t=4)
+            copy(wd_bf[a][:, :, m0 : m0 + src.shape[1], :].rearrange("p t m i -> p m i t"), src)
 
         def quant_wd(a):
-            if a == 0:
-                codes = shared.tile([P, H], U32, name="got", align_bytes=64, offset=12800)
-            else:
-                codes = keep.tile([P, H], U32, name=f"wd_codes{a}", align_bytes=64)
-            scale = keep.tile([P, H], U8, name=f"wd_scale{a}", align_bytes=64)
+            wd_codes[a] = kept([P, H], U32, f"wd_codes{a}")
+            wd_scale[a] = kept([P, H], U8, f"wd_scale{a}")
             nc.vector.quantize_mx(
-                out=codes[:].bitcast(FP8X4), scales=scale[:], in_=wd_bf[a][:].rearrange("p t m i -> p (t m i)")
-            )
-            wd_codes.append(codes)
-            wd_scale.append(scale)
-
-        c_acc = [[psum.tile([P, HALF], F32, name="acc") for t in range(4)] for b in range(2)]
-
-        def c_pass(a, b, t):
-            rhs, rhs_scale = v_operand(a, HALF * b, HALF)
-            nc.tensor.matmul_mx(
-                out=c_acc[b][t][:],
-                lhsT=wc_codes[a // 2][:, a % 2, P * t : P * (t + 1)].bitcast(FP4X4),
-                lhsT_scale=planes[:, a, WC0 + P * t : WC0 + P * (t + 1)],
-                rhs=rhs,
-                rhs_scale=rhs_scale,
-                start=(a == 0),
-                stop=(a == PASSES - 1),
+                out=wd_codes[a][:].bitcast(FP8X4),
+                scales=wd_scale[a][:],
+                in_=wd_bf[a][:].rearrange("p t m i -> p (t m i)"),
             )
 
-        order_wc(0)
-        load_wd(0, "wc_raw0")
-        g00 = gather_words(0, 0)
-        part_words(0, 0, g00)
-        got_scale_b = shared.tile([P, HALF], U8, name="got_scale_b", align_bytes=64, offset=12288)
-        nc.vector.tensor_copy(got_scale_b[:], tab_scale[:].indirect(offsets[:, 32:64]))
-        for q in range(4):
-            (nc.sync, nc.scalar)[q // 2].dma_start(
-                words(planes_b[32 * q : 32 * q + 4]), got_scale_b[16 * q : 16 * q + 16, :].bitcast(I32)
-            )
-        load_wd(1, "tab_scale")
-        order_wc(1)
-        load_wd(2, "wc_raw1")
-        for a in range(2):
+        c_acc = [[bank([P, HALF], 4 * b + t) for t in range(4)] for b in range(2)]
+
+        def c_passes(m, b):
             for t in range(4):
-                c_pass(a, 0, t)
-        part_words(1, 0, gather_words(1, 0))
-        cast_wd(0, False)
-        load_wd(3, "wc_raw0")
-        for t in range(4):
-            c_pass(2, 0, t)
-            c_pass(3, 0, t)
-        part_words(0, 1, gather_words(0, 1))
-        for a in range(2):
-            for t in range(4):
-                c_pass(a, 1, t)
-        part_words(1, 1, gather_words(1, 1))
-        cast_wd(1, False)
-        for t in range(4):
-            c_pass(2, 1, t)
-            c_pass(3, 1, t)
+                for a in (2 * m, 2 * m + 1):
+                    rhs, rhs_scale = v_operand(a, HALF * b, HALF)
+                    nc.tensor.matmul_mx(
+                        out=c_acc[b][t][:],
+                        lhsT=wc_codes[m][:, a % 2, P * t : P * (t + 1)].bitcast(FP4X4),
+                        lhsT_scale=planes[0][:, a, HALF + P * t : HALF + P * (t + 1)],
+                        rhs=rhs,
+                        rhs_scale=rhs_scale,
+                        start=(a == 0),
+                        stop=(a == PASSES - 1),
+                    )
+
+        order_wc(0, kept([P, 2, H], U16, "wc_codes0"))
+        gather_words(0, 0, placed([P, HALF], U32, "got_first", 41984))
+        part_words(0, 0)
+        c_passes(0, 0)
+        gather_words(0, 1, placed([P, HALF], U32, "got0", 43008))
+        order_wc(1, placed([P, 2, H], U16, "wc_codes1", 40960))
+        part_words(0, 1)
+        c_passes(0, 1)
+        for half in range(2):
+            cast_wd(0, wd0_raw[half], 64 * half, nc.scalar.copy)
+        gather_words(1, 0, kept([P, HALF], U32, "got1"))
+        gather_words(1, 1, placed([P, HALF], U32, "got0", 43008))
+        part_words(1, 0)
+        part_words(1, 1)
+        c_passes(1, 0)
+        c_passes(1, 1)
+
+        wos = kept([P, N], U8, "tab_words0")
+        nc.vector.memset(wos[:].bitcast(I32), 0)
+        for r in range(4):
+            nc.sync.dma_start(wos[r:P:32, :].bitcast(I32), wo_scales[0, r:16:4, :].bitcast(I32))
+        rate_sb = kept([P, NT], F32, "got1")
+        with nc.allow_non_contiguous_dma(reason="one rate for each output row"):
+            nc.sync.dma_start(rate_sb[:], rate.rearrange("(u p) -> p u", p=P))
+
+        cast_wd(1, wd_raw[1], 0, nc.vector.tensor_copy)
         quant_wd(0)
+        cast_wd(2, wd_raw[2], 0, nc.vector.tensor_copy)
+        quant_wd(1)
+        cast_wd(3, wd_raw[3], 0, nc.vector.tensor_copy)
+        quant_wd(2)
+        quant_wd(3)
 
-        sq = [keep.tile([P, 4, HALF], F32, name=room, align_bytes=64) for room in ("tab_scale", "sq1")]
-        damp = [keep.tile([P, CHUNK, 4], F32, name=f"damp{i}") for i in range(S // CHUNK)]
+        sq = [kept([P, 4, HALF], F32, f"sq{b}") for b in range(2)]
+        damp = [kept([P, PAIR, 4], F32, f"damp{g}") for g in range(S // PAIR)]
 
-        def square(b, t):
-            nc.scalar.activation(sq[b][:, t, :], c_acc[b][t][:], ACT.Square)
+        def squares(b):
+            for t in range(4):
+                nc.scalar.activation(sq[b][:, t, :], c_acc[b][t][:], ACT.Square)
 
-        def rsqrt(i):
-            b, o = divmod(CHUNK * i, HALF)
+        def rsqrt(g):
+            b, o = divmod(PAIR * g, HALF)
             nc.scalar.activation(
-                damp[i][:].rearrange("p (c e) t -> p c t e", e=4),
-                sq[b][:, :, o : o + CHUNK].rearrange("p t (c e) -> p c t e", e=4),
+                damp[g][:].rearrange("p (c e) t -> p c t e", e=4),
+                sq[b][:, :, o : o + PAIR].rearrange("p t (c e) -> p c t e", e=4),
                 ACT.Abs_reciprocal_sqrt,
                 bias=1.0,
             )
 
-        for t in range(4):
-            square(0, t)
-        cast_wd(2, True)
-        quant_wd(1)
-        wos = keep.tile([P, N], U8, name="tab_words0", align_bytes=64)
-        nc.gpsimd.memset(wos[:].bitcast(I32), 0)
-        for r in range(4):
-            nc.sync.dma_start(wos[r:P:32, :].bitcast(I32), wo_scales[0, r:16:4, :].bitcast(I32))
-        rate_sb = keep.tile([P, NT], F32, name="wc_raw1", align_bytes=64)
-        with nc.allow_non_contiguous_dma(reason="one rate for each output row"):
-            nc.sync.dma_start(rate_sb[:], rate.rearrange("(u p) -> p u", p=P))
-        quant_wd(2)
-        cast_wd(3, True)
-        for i in range(2):
-            rsqrt(i)
-        for t in range(4):
-            square(1, t)
-        for i in range(2, 4):
-            rsqrt(i)
-        quant_wd(3)
+        squares(0)
+        rsqrt(0)
+        squares(1)
+        for g in range(1, 4):
+            rsqrt(g)
 
         d_acc = {}
 
-        def d_pass(a, i):
+        def d_pass(a, i, b):
             if a == 0:
-                d_acc[i] = psum.tile([P, 4, CHUNK], F32, name="acc")
+                d_acc[i] = bank([P, 4, CHUNK], b)
             rhs, rhs_scale = v_operand(a, CHUNK * i, CHUNK)
             for t in range(4):
                 nc.tensor.matmul_mx(
@@ -263,67 +241,84 @@ def tile_list_momentum_block_steps_kernel(
                     stop=(a == PASSES - 1 and t == 3),
                 )
 
-        h_bf, h_codes, h_scale = {}, {}, {}
+        def d_chunk(i):
+            for a in range(PASSES):
+                d_pass(a, i, i % 2)
+
+        h_bf = [kept([P, 2, CHUNK, 4], BF16, f"h_bf{g}") for g in range(S // PAIR)]
+        h_codes = [kept([P, HALF], U32, f"h_codes{b}") for b in range(2)]
+        h_scale = [kept([P, HALF], U8, f"h_scale{b}") for b in range(2)]
 
         def damp_chunk(i):
-            g = i // 2
-            if i % 2 == 0:
-                h_bf[g] = ring.tile([P, 2, CHUNK, 4], BF16, name="h_bf", align_bytes=64)
+            g, e = divmod(i, 2)
             nc.vector.tensor_tensor(
-                h_bf[g][:, i % 2], d_acc[i][:].rearrange("p t n -> p n t"), damp[i][:], MULT
+                h_bf[g][:, e], d_acc[i][:].rearrange("p t n -> p n t"), damp[g][:, CHUNK * e : CHUNK * (e + 1), :], MULT
             )
 
         def quant_h(g):
-            h_codes[g] = ring.tile([P, PAIR], U32, name="h_codes", align_bytes=64)
-            h_scale[g] = ring.tile([P, PAIR], U8, name="h_scale", align_bytes=64)
+            b, o = divmod(PAIR * g, HALF)
             nc.vector.quantize_mx(
-                out=h_codes[g][:].bitcast(FP8X4),
-                scales=h_scale[g][:],
+                out=h_codes[b][:, o : o + PAIR].bitcast(FP8X4),
+                scales=h_scale[b][:, o : o + PAIR],
                 in_=h_bf[g][:].rearrange("p c n t -> p (c n t)"),
             )
 
-        def step_out(g):
+        def y_pass(acc, u, c0, width):
+            b, o = divmod(c0, HALF)
+            nc.tensor.matmul_mx(
+                out=acc,
+                lhsT=wo_codes[:, P * u : P * (u + 1)].bitcast(FP8X4),
+                lhsT_scale=wos[:, P * u : P * (u + 1)],
+                rhs=h_codes[b][:, o : o + width].bitcast(FP8X4),
+                rhs_scale=h_scale[b][:, o : o + width],
+                start=True,
+                stop=True,
+            )
+
+        def out_first_half(banks):
+            for u in range(NT):
+                acc = bank([P, HALF], banks[u])
+                y_pass(acc[:], u, 0, HALF)
+                res = kept([P, HALF], F32, f"res_a{u}")
+                nc.scalar.activation(res[:], acc[:], ACT.Copy, scale=rate_sb[:, u : u + 1])
+                nc.sync.dma_start(out[P * u : P * (u + 1), 0:HALF], res[:])
+
+        def out_pair(g, banks, on_vector):
             for bk in range(NT // 2):
-                acc = psum.tile([P, 2, PAIR], F32, name="acc")
+                acc = bank([P, 2, PAIR], banks[bk])
                 for e in range(2):
-                    u = 2 * bk + e
-                    nc.tensor.matmul_mx(
-                        out=acc[:, e, :],
-                        lhsT=wo_codes[:, P * u : P * (u + 1)].bitcast(FP8X4),
-                        lhsT_scale=wos[:, P * u : P * (u + 1)],
-                        rhs=h_codes[g][:].bitcast(FP8X4),
-                        rhs_scale=h_scale[g][:],
-                        start=True,
-                        stop=True,
-                    )
-                res = outp.tile([P, 2, PAIR], F32, name="res")
-                for e in range(2):
-                    u = 2 * bk + e
-                    if bk == 1:
-                        nc.vector.tensor_scalar(res[:, e, :], acc[:, e, :], rate_sb[:, u : u + 1], None, MULT)
-                    else:
+                    y_pass(acc[:, e, :], 2 * bk + e, PAIR * g, PAIR)
+                res = kept([P, 2, PAIR], F32, f"res{g}_{bk}")
+                if on_vector:
+                    rates = rate_sb[:, 2 * bk : 2 * bk + 2].unsqueeze(2).to_broadcast([P, 2, PAIR])
+                    nc.vector.tensor_tensor(res[:], acc[:], rates, MULT)
+                else:
+                    for e in range(2):
+                        u = 2 * bk + e
                         nc.scalar.activation(res[:, e, :], acc[:, e, :], ACT.Copy, scale=rate_sb[:, u : u + 1])
                 nc.sync.dma_start(
                     out[2 * P * bk : 2 * P * (bk + 1), PAIR * g : PAIR * (g + 1)].rearrange("(e p) j -> p e j", p=P),
                     res[:],
                 )
 
-        for a in range(PASSES - 1):
+        for a in range(PASSES):
             for i in range(4):
-                d_pass(a, i)
-        for i in range(4):
-            d_pass(PASSES - 1, i)
+                d_pass(a, i, i)
+        for i in range(3):
             damp_chunk(i)
-            if i % 2 == 1:
-                quant_h(i // 2)
-        for i in range(4, 8):
-            rsqrt(i)
-        for i in range(4, 8):
-            for a in range(PASSES):
-                d_pass(a, i)
-            damp_chunk(i)
-            if i % 2 == 1:
-                quant_h(i // 2)
-            if i < 7:
-                step_out(i - 4) if i < 6 else step_out(2)
-        step_out(3)
+        quant_h(0)
+        damp_chunk(3)
+        quant_h(1)
+        d_chunk(4)
+        d_chunk(5)
+        out_first_half((4, 5, 6, 7, 2, 3))
+        damp_chunk(4)
+        damp_chunk(5)
+        quant_h(2)
+        d_chunk(6)
+        d_chunk(7)
+        out_pair(2, (4, 5, 6), False)
+        damp_chunk(6)
+        damp_chunk(7)
+        quant_h(3)
+        out_pair(3, (7, 2, 3), True)

@@ -75,15 +75,15 @@ def tile_list_momentum_block_steps_kernel(
             nc.sync.dma_start(tile[:].bitcast(I32), tab[m, 0 : 512 * T].rearrange("(p w) -> p w", p=P).bitcast(I32))
             return tile
 
-        def load_wd(a, raw, r0):
-            rows = wd[512 * a : 512 * (a + 1), r0 : r0 + raw.shape[2]]
-            nc.sync.dma_start(raw[:], rows.rearrange("(p i) r -> p i r", i=4))
+        def load_wd(a, raw, i0):
+            rows = wd[512 * a : 512 * (a + 1), :].rearrange("(p i) r -> p i r", i=4)
+            nc.sync.dma_start(raw[:], rows[:, i0 : i0 + raw.shape[1], :])
             return raw
 
         load_wc(0)
         tab_words = [load_tab(0, kept([P, T], U32, "tab_words0"))]
         load_wc(1)
-        wd0_raw = [load_wd(0, kept([P, 4, H // 2], F32, "wd0_raw0"), 0)]
+        wd0_raw = [load_wd(0, kept([P, 2, H], F32, "wd0_raw0"), 0)]
 
         got_a = placed([P, HALF], U8, "got_a", 3072)
         nc.vector.tensor_copy(got_a[:], tab_scale[:].indirect(offsets[:, 0:32]))
@@ -102,7 +102,7 @@ def tile_list_momentum_block_steps_kernel(
         nc.vector.tensor_copy(got_b[:], tab_scale[:].indirect(offsets[:, 32:64]))
         for q in (0, 2, 1, 3):
             nc.scalar.dma_start(words(planes[1][32 * q : 32 * q + 4]), got_b[16 * q : 16 * q + 16, :].bitcast(I32))
-        wd0_raw.append(load_wd(0, placed([P, 4, H // 2], F32, "wd0_raw1", 11520), H // 2))
+        wd0_raw.append(load_wd(0, placed([P, 2, H], F32, "wd0_raw1", 11520), 2))
         wd_raw = {
             1: load_wd(1, placed([P, 4, H], F32, "wd_raw1", 16384), 0),
             2: load_wd(2, placed([P, 4, H], F32, "wd_raw2", 24576), 0),
@@ -140,9 +140,9 @@ def tile_list_momentum_block_steps_kernel(
         wd_bf = [kept([P, 4, P, 4], BF16, f"wd_bf{a}") for a in range(PASSES)]
         wd_codes, wd_scale = {}, {}
 
-        def cast_wd(a, raw, m0, copy):
+        def cast_wd(a, raw, i0, copy):
             src = raw[:].rearrange("p i (m t) -> p m i t", t=4)
-            copy(wd_bf[a][:, :, m0 : m0 + src.shape[1], :].rearrange("p t m i -> p m i t"), src)
+            copy(wd_bf[a][:, :, :, i0 : i0 + raw.shape[1]].rearrange("p t m i -> p m i t"), src)
 
         def quant_wd(a):
             wd_codes[a] = kept([P, H], U32, f"wd_codes{a}")
@@ -178,7 +178,7 @@ def tile_list_momentum_block_steps_kernel(
         part_words(0, 1)
         c_passes(0, 1)
         for half in range(2):
-            cast_wd(0, wd0_raw[half], 64 * half, nc.scalar.copy)
+            cast_wd(0, wd0_raw[half], 2 * half, nc.scalar.copy)
         gather_words(1, 0, kept([P, HALF], U32, "got1"))
         gather_words(1, 1, placed([P, HALF], U32, "got0", 43008))
         part_words(1, 0)
@@ -194,13 +194,10 @@ def tile_list_momentum_block_steps_kernel(
         with nc.allow_non_contiguous_dma(reason="one rate for each output row"):
             nc.sync.dma_start(rate_sb[:], rate.rearrange("(u p) -> p u", p=P))
 
-        cast_wd(1, wd_raw[1], 0, nc.vector.tensor_copy)
         quant_wd(0)
-        cast_wd(2, wd_raw[2], 0, nc.vector.tensor_copy)
-        quant_wd(1)
-        cast_wd(3, wd_raw[3], 0, nc.vector.tensor_copy)
-        quant_wd(2)
-        quant_wd(3)
+        for a in range(1, PASSES):
+            cast_wd(a, wd_raw[a], 0, nc.vector.tensor_copy)
+            quant_wd(a)
 
         sq = [kept([P, 4, HALF], F32, f"sq{b}") for b in range(2)]
         damp = [kept([P, PAIR, 4], F32, f"damp{g}") for g in range(S // PAIR)]
@@ -255,12 +252,13 @@ def tile_list_momentum_block_steps_kernel(
                 h_bf[g][:, e], d_acc[i][:].rearrange("p t n -> p n t"), damp[g][:, CHUNK * e : CHUNK * (e + 1), :], MULT
             )
 
-        def quant_h(g):
-            b, o = divmod(PAIR * g, HALF)
+        def quant_h(i, chunks):
+            g, e = divmod(i, 2)
+            b, o = divmod(CHUNK * i, HALF)
             nc.vector.quantize_mx(
-                out=h_codes[b][:, o : o + PAIR].bitcast(FP8X4),
-                scales=h_scale[b][:, o : o + PAIR],
-                in_=h_bf[g][:].rearrange("p c n t -> p (c n t)"),
+                out=h_codes[b][:, o : o + CHUNK * chunks].bitcast(FP8X4),
+                scales=h_scale[b][:, o : o + CHUNK * chunks],
+                in_=h_bf[g][:, e : e + chunks].rearrange("p c n t -> p (c n t)"),
             )
 
         def y_pass(acc, u, c0, width):
@@ -280,16 +278,20 @@ def tile_list_momentum_block_steps_kernel(
                 acc = bank([P, HALF], banks[u])
                 y_pass(acc[:], u, 0, HALF)
                 res = kept([P, HALF], F32, f"res_a{u}")
-                nc.scalar.activation(res[:], acc[:], ACT.Copy, scale=rate_sb[:, u : u + 1])
+                if u >= 5:
+                    nc.vector.tensor_scalar(res[:], acc[:], rate_sb[:, u : u + 1], None, MULT)
+                else:
+                    nc.scalar.activation(res[:], acc[:], ACT.Copy, scale=rate_sb[:, u : u + 1])
                 nc.sync.dma_start(out[P * u : P * (u + 1), 0:HALF], res[:])
 
-        def out_pair(g, banks, on_vector):
-            for bk in range(NT // 2):
-                acc = bank([P, 2, PAIR], banks[bk])
-                for e in range(2):
-                    y_pass(acc[:, e, :], 2 * bk + e, PAIR * g, PAIR)
+        def out_pair(g, banks, on_vector, width):
+            accs = [bank([P, 2, PAIR], b) for b in banks]
+            for o in range(0, PAIR, width):
+                for u in range(NT):
+                    y_pass(accs[u // 2][:, u % 2, o : o + width], u, PAIR * g + o, width)
+            for bk, acc in enumerate(accs):
                 res = kept([P, 2, PAIR], F32, f"res{g}_{bk}")
-                if on_vector:
+                if bk in on_vector:
                     rates = rate_sb[:, 2 * bk : 2 * bk + 2].unsqueeze(2).to_broadcast([P, 2, PAIR])
                     nc.vector.tensor_tensor(res[:], acc[:], rates, MULT)
                 else:
@@ -306,19 +308,19 @@ def tile_list_momentum_block_steps_kernel(
                 d_pass(a, i, i)
         for i in range(3):
             damp_chunk(i)
-        quant_h(0)
+        quant_h(0, 2)
         damp_chunk(3)
-        quant_h(1)
+        quant_h(2, 2)
         d_chunk(4)
         d_chunk(5)
-        out_first_half((4, 5, 6, 7, 2, 3))
         damp_chunk(4)
         damp_chunk(5)
-        quant_h(2)
+        quant_h(4, 2)
+        out_first_half((4, 5, 6, 7, 2, 3))
         d_chunk(6)
+        out_pair(2, (4, 5, 6), (), PAIR)
         d_chunk(7)
-        out_pair(2, (4, 5, 6), False)
-        damp_chunk(6)
-        damp_chunk(7)
-        quant_h(3)
-        out_pair(3, (7, 2, 3), True)
+        for i in (6, 7):
+            damp_chunk(i)
+            quant_h(i, 1)
+        out_pair(3, (7, 2, 3), (0, 2), CHUNK)

@@ -223,8 +223,8 @@ def tile_list_momentum_block_steps_kernel(
 
         d_acc = {}
 
-        def d_pass(a, i, b):
-            if a == 0:
+        def d_pass(a, i, b, first=0, last=PASSES - 1):
+            if a == first:
                 d_acc[i] = bank([P, 4, CHUNK], b)
             rhs, rhs_scale = v_operand(a, CHUNK * i, CHUNK)
             for t in range(4):
@@ -234,13 +234,13 @@ def tile_list_momentum_block_steps_kernel(
                     lhsT_scale=wd_scale[a][:, P * t : P * (t + 1)],
                     rhs=rhs,
                     rhs_scale=rhs_scale,
-                    start=(a == 0 and t == 0),
-                    stop=(a == PASSES - 1 and t == 3),
+                    start=(a == first and t == 0),
+                    stop=(a == last and t == 3),
                 )
 
         def d_chunk(i):
-            for a in range(PASSES):
-                d_pass(a, i, i % 2)
+            for a in reversed(range(PASSES)):
+                d_pass(a, i, i, PASSES - 1, 0)
 
         h_bf = [kept([P, 2, CHUNK, 4], BF16, f"h_bf{g}") for g in range(S // PAIR)]
         h_codes = [kept([P, HALF], U32, f"h_codes{b}") for b in range(2)]
@@ -273,54 +273,66 @@ def tile_list_momentum_block_steps_kernel(
                 stop=True,
             )
 
-        def out_first_half(banks):
+        def y_cols(c0, width, banks):
+            per_bank = NT // len(banks)
+            accs = [bank([P, per_bank, width], b) for b in banks]
             for u in range(NT):
-                acc = bank([P, HALF], banks[u])
-                y_pass(acc[:], u, 0, HALF)
-                res = kept([P, HALF], F32, f"res_a{u}")
-                if u >= 5:
-                    nc.vector.tensor_scalar(res[:], acc[:], rate_sb[:, u : u + 1], None, MULT)
-                else:
-                    nc.scalar.activation(res[:], acc[:], ACT.Copy, scale=rate_sb[:, u : u + 1])
-                nc.sync.dma_start(out[P * u : P * (u + 1), 0:HALF], res[:])
+                y_pass(accs[u // per_bank][:, u % per_bank, :], u, c0, width)
+            return [(acc, per_bank * bk, c0) for bk, acc in enumerate(accs)]
 
-        def out_pair(g, banks, on_vector, width):
-            accs = [bank([P, 2, PAIR], b) for b in banks]
-            for o in range(0, PAIR, width):
-                for u in range(NT):
-                    y_pass(accs[u // 2][:, u % 2, o : o + width], u, PAIR * g + o, width)
-            for bk, acc in enumerate(accs):
-                res = kept([P, 2, PAIR], F32, f"res{g}_{bk}")
-                if bk in on_vector:
-                    rates = rate_sb[:, 2 * bk : 2 * bk + 2].unsqueeze(2).to_broadcast([P, 2, PAIR])
-                    nc.vector.tensor_tensor(res[:], acc[:], rates, MULT)
-                else:
-                    for e in range(2):
-                        u = 2 * bk + e
-                        nc.scalar.activation(res[:, e, :], acc[:, e, :], ACT.Copy, scale=rate_sb[:, u : u + 1])
-                nc.sync.dma_start(
-                    out[2 * P * bk : 2 * P * (bk + 1), PAIR * g : PAIR * (g + 1)].rearrange("(e p) j -> p e j", p=P),
-                    res[:],
-                )
+        def store(res, u0, c0):
+            rows, width = res.shape[1], res.shape[2]
+            nc.sync.dma_start(out[P * u0 : P * (u0 + rows), c0 : c0 + width].rearrange("(e p) j -> p e j", p=P), res[:])
 
-        for a in range(PASSES):
+        def empty_on_vector(acc, u0, c0):
+            res = kept(acc.shape, F32, f"res{c0}_{u0}")
+            rates = rate_sb[:, u0 : u0 + acc.shape[1]].unsqueeze(2).to_broadcast(acc.shape)
+            nc.vector.tensor_tensor(res[:], acc[:], rates, MULT)
+            store(res, u0, c0)
+
+        def empty_on_scalar(acc, u0, c0):
+            res = kept(acc.shape, F32, f"res{c0}_{u0}")
+            for e in range(acc.shape[1]):
+                nc.scalar.activation(res[:, e, :], acc[:, e, :], ACT.Copy, scale=rate_sb[:, u0 + e : u0 + e + 1])
+            store(res, u0, c0)
+
+        for i in range(4):
+            for a in (0, 1):
+                d_pass(a, i, i)
+        for a in (2, 3):
             for i in range(4):
                 d_pass(a, i, i)
+        d_chunk(4)
         for i in range(3):
             damp_chunk(i)
         quant_h(0, 2)
-        damp_chunk(3)
-        quant_h(2, 2)
-        d_chunk(4)
+        pair0 = y_cols(0, PAIR, (0, 1, 2))
+        empty_on_scalar(*pair0[0])
         d_chunk(5)
+        damp_chunk(3)
         damp_chunk(4)
+        quant_h(2, 2)
+        empty_on_vector(*pair0[1])
+        pair1 = y_cols(PAIR, PAIR, (3, 4, 0))
+        empty_on_scalar(*pair1[0])
+        d_chunk(6)
         damp_chunk(5)
         quant_h(4, 2)
-        out_first_half((4, 5, 6, 7, 2, 3))
-        d_chunk(6)
-        out_pair(2, (4, 5, 6), (), PAIR)
+        empty_on_vector(*pair0[2])
+        damp_chunk(6)
+        quant_h(6, 1)
+        empty_on_scalar(*pair1[1])
+        pair2 = y_cols(2 * PAIR, PAIR, (1, 2, 5))
+        empty_on_vector(*pair1[2])
         d_chunk(7)
-        for i in (6, 7):
-            damp_chunk(i)
-            quant_h(i, 1)
-        out_pair(3, (7, 2, 3), (0, 2), CHUNK)
+        empty_on_scalar(*pair2[0])
+        empty_on_scalar(*pair2[1])
+        last_but_one = y_cols(6 * CHUNK, CHUNK, (6, 3))
+        damp_chunk(7)
+        quant_h(7, 1)
+        empty_on_vector(*pair2[2])
+        empty_on_scalar(*last_but_one[0])
+        last = y_cols(7 * CHUNK, CHUNK, (4, 0))
+        empty_on_vector(*last_but_one[1])
+        empty_on_scalar(*last[0])
+        empty_on_vector(*last[1])

@@ -23,6 +23,7 @@ CHUNK = 128
 PAIR = 256
 NT = N // P
 ROW = HALF + H
+RUN = 2
 
 
 def tile_list_momentum_block_steps_kernel(
@@ -200,7 +201,7 @@ def tile_list_momentum_block_steps_kernel(
             quant_wd(a)
 
         sq = [kept([P, 4, HALF], F32, f"sq{b}") for b in range(2)]
-        damp = [kept([P, PAIR, 4], F32, f"damp{g}") for g in range(S // PAIR)]
+        damp = [kept([P, PAIR // RUN, 4, RUN], F32, f"damp{g}") for g in range(S // PAIR)]
 
         def squares(b):
             for t in range(4):
@@ -209,8 +210,8 @@ def tile_list_momentum_block_steps_kernel(
         def rsqrt(g):
             b, o = divmod(PAIR * g, HALF)
             nc.scalar.activation(
-                damp[g][:].rearrange("p (c e) t -> p c t e", e=4),
-                sq[b][:, :, o : o + PAIR].rearrange("p t (c e) -> p c t e", e=4),
+                damp[g][:],
+                sq[b][:, :, o : o + PAIR].rearrange("p t (c e) -> p c t e", e=RUN),
                 ACT.Abs_reciprocal_sqrt,
                 bias=1.0,
             )
@@ -248,8 +249,12 @@ def tile_list_momentum_block_steps_kernel(
 
         def damp_chunk(i):
             g, e = divmod(i, 2)
+            runs = CHUNK // RUN
             nc.vector.tensor_tensor(
-                h_bf[g][:, e], d_acc[i][:].rearrange("p t n -> p n t"), damp[g][:, CHUNK * e : CHUNK * (e + 1), :], MULT
+                h_bf[g][:, e].rearrange("p (c n) t -> p c t n", n=RUN),
+                d_acc[i][:].rearrange("p t (c n) -> p c t n", n=RUN),
+                damp[g][:, runs * e : runs * (e + 1)],
+                MULT,
             )
 
         def quant_h(i, chunks):

@@ -22,7 +22,11 @@ HALF = 512
 CHUNK = 128
 PAIR = 256
 NT = N // P
-ROW = HALF + H
+ROW = HALF + H + HALF
+TAB1 = 10240
+GOT = TAB1 + 10240
+LATE = GOT + 8192
+LAST = LATE + 16384
 RUN = 2
 
 
@@ -48,26 +52,31 @@ def tile_list_momentum_block_steps_kernel(
             return tile.rearrange("p a e -> p (a e)").bitcast(I32).rearrange("p (a e) -> p a e", a=tile.shape[1])
 
         offsets = keep.tile([P, S // 16], U16, name="offsets")
-        tab_scale = placed([P, T], U8, "tab_scale", 15360)
+        tab_scale = kept([P, T], U8, "tab_scale")
         wcs_raw = kept([P, H], U8, "wcs_raw")
-        wc_raw = [kept([P, 2, H], U16, f"wc_raw{m}") for m in range(2)]
-        planes = [kept([P, 4, ROW], U8, "planes_a"), kept([P, 4, HALF], U8, "planes_b")]
+        wc_raw = [kept([P, 2, H], U16, "wc_raw0"), placed([P, 2, H], U16, "wc_raw1", LATE + 7168)]
+        first_planes = kept([P, 2, HALF + H], U8, "first_planes")
+        second_planes = kept([P, 2, HALF], U8, "second_planes")
+        late_planes = kept([P, 2, ROW], U8, "late_planes")
         warm = keep.tile([P, 2], F32, name="warm")
 
         nc.vector.memset(warm[:, 0:1], 1.0)
         nc.scalar.activation(warm[:, 1:2], warm[:, 0:1], ACT.Abs_reciprocal_sqrt, bias=1.0)
         nc.vector.memset(tab_scale[64:128, :].bitcast(I32), 0)
         nc.vector.memset(wcs_raw[64:128, :].bitcast(I32), 0)
-        for b in range(2):
-            nc.vector.memset(planes[b][:].rearrange("p a e -> p (a e)").bitcast(I32), 0)
+        for plane in (first_planes, second_planes, late_planes):
+            nc.vector.memset(plane[:].rearrange("p a e -> p (a e)").bitcast(I32), 0)
 
         nc.sync.dma_start(offsets[:], offs)
         for m in range(2):
             nc.sync.dma_start(
-                tab_scale[m:64:2, :].bitcast(I32),
+                wcs_raw[32 * m : 32 * (m + 1), :].bitcast(I32), wc_scales.bitcast(I32)[2 * m : 2 * m + 2].rearrange("h q e -> q h e")
+            )
+        for m in range(2):
+            nc.sync.dma_start(
+                tab_scale[32 * m : 32 * (m + 1), :].bitcast(I32),
                 tab[m, 512 * T :].rearrange("(h q t) -> q h t", h=2, q=16).bitcast(I32),
             )
-        nc.scalar.dma_start(wcs_raw[0:64, :].bitcast(I32), wc_scales.bitcast(I32).rearrange("a q e -> q a e"))
 
         def load_wc(m):
             nc.sync.dma_start(words(wc_raw[m][:]), wc_words.bitcast(I32)[2 * m : 2 * m + 2].rearrange("a p e -> p a e"))
@@ -76,42 +85,44 @@ def tile_list_momentum_block_steps_kernel(
             nc.sync.dma_start(tile[:].bitcast(I32), tab[m, 0 : 512 * T].rearrange("(p w) -> p w", p=P).bitcast(I32))
             return tile
 
-        def load_wd(a, raw, i0):
+        def load_wd(a, raw, c0):
             rows = wd[512 * a : 512 * (a + 1), :].rearrange("(p i) r -> p i r", i=4)
-            nc.sync.dma_start(raw[:], rows[:, i0 : i0 + raw.shape[1], :])
-            return raw
+            nc.sync.dma_start(raw[:], rows[:, :, c0 : c0 + raw.shape[2]])
+            return raw, c0
+
+        def move_rows(plane, rows, m, queues):
+            for q in (0, 2, 1, 3):
+                queues[q // 2].dma_start(
+                    words(plane[32 * q : 32 * q + 4]), rows[32 * m + 8 * q : 32 * m + 8 * (q + 1), :].bitcast(I32)
+                )
 
         load_wc(0)
         tab_words = [load_tab(0, kept([P, T], U32, "tab_words0"))]
         load_wc(1)
-        wd0_raw = [load_wd(0, kept([P, 2, H], F32, "wd0_raw0"), 0)]
+        wd_parts = {0: [load_wd(0, kept([P, 4, H // 2], F32, "wd0_left"), 0)]}
 
-        got_a = placed([P, HALF], U8, "got_a", 3072)
+        stage = placed([P, ROW], U8, "stage", LAST + 3328)
+        got_a = placed([P, HALF], U8, "got_a", TAB1)
         nc.vector.tensor_copy(got_a[:], tab_scale[:].indirect(offsets[:, 0:32]))
-        stage = placed([P, ROW], U8, "stage", 32256)
         nc.vector.tensor_copy(
-            stage[:, HALF:ROW].rearrange("p (t c i) -> p c t i", t=4, i=16),
+            stage[:, HALF : HALF + H].rearrange("p (t c i) -> p c t i", t=4, i=16),
             wcs_raw[:].rearrange("p (c i t) -> p c t i", t=4, i=16),
         )
         nc.vector.tensor_copy(stage[0:64, 0:HALF].bitcast(I32), got_a[0:64, :].bitcast(I32))
-        for q in range(4):
-            (nc.sync, nc.scalar)[q // 2].dma_start(
-                words(planes[0][32 * q : 32 * q + 4]), stage[16 * q : 16 * q + 16, :].bitcast(I32)
-            )
-        tab_words.append(load_tab(1, placed([P, T], U32, "tab_words1", 3328)))
-        got_b = placed([P, HALF], U8, "got_b", 2816)
+        move_rows(first_planes, stage[:, 0 : HALF + H], 0, (nc.sync, nc.scalar))
+        tab_words.append(load_tab(1, placed([P, T], U32, "tab_words1", TAB1 + 256)))
+        got_b = placed([P, HALF], U8, "got_b", TAB1 - 256)
         nc.vector.tensor_copy(got_b[:], tab_scale[:].indirect(offsets[:, 32:64]))
-        for q in (0, 2, 1, 3):
-            nc.scalar.dma_start(words(planes[1][32 * q : 32 * q + 4]), got_b[16 * q : 16 * q + 16, :].bitcast(I32))
-        wd0_raw.append(load_wd(0, placed([P, 2, H], F32, "wd0_raw1", 11520), 2))
-        wd_raw = {
-            1: load_wd(1, placed([P, 4, H], F32, "wd_raw1", 16384), 0),
-            2: load_wd(2, placed([P, 4, H], F32, "wd_raw2", 24576), 0),
-            3: load_wd(3, placed([P, 4, H], F32, "wd_raw3", 32768), 0),
-        }
-        wo_codes = placed([P, N], U32, "wo_codes", 0)
-        nc.sync.dma_start(wo_codes[:].bitcast(I32), wo_words[0].rearrange("p e i -> p (e i)").bitcast(I32))
+        move_rows(second_planes, got_b, 0, (nc.sync, nc.sync))
+        nc.vector.tensor_copy(stage[0:64, HALF + H : ROW].bitcast(I32), got_b[0:64, :].bitcast(I32))
+        move_rows(late_planes, stage, 1, (nc.sync, nc.sync))
+        wd_parts[0].append(load_wd(0, placed([P, 4, H // 2], F32, "wd0_right", TAB1 - 4096), H // 2))
 
+        table_planes = [
+            [first_planes[:, :, 0:HALF], second_planes],
+            [late_planes[:, :, 0:HALF], late_planes[:, :, HALF + H : ROW]],
+        ]
+        wc_planes = [plane[:, :, HALF : HALF + H] for plane in (first_planes, late_planes)]
         wc_codes, got, v_codes = {}, {}, {}
 
         def order_wc(m, codes):
@@ -136,14 +147,15 @@ def tile_list_momentum_block_steps_kernel(
         def v_operand(a, c0, width):
             m, h = divmod(a, 2)
             b, o = divmod(c0, HALF)
-            return v_codes[(m, b)][:, h, o : o + width].bitcast(FP4X4), planes[b][:, 2 * h + m, o : o + width]
+            return v_codes[(m, b)][:, h, o : o + width].bitcast(FP4X4), table_planes[m][b][:, h, o : o + width]
 
         wd_bf = [kept([P, 4, P, 4], BF16, f"wd_bf{a}") for a in range(PASSES)]
         wd_codes, wd_scale = {}, {}
 
-        def cast_wd(a, raw, i0, copy):
-            src = raw[:].rearrange("p i (m t) -> p m i t", t=4)
-            copy(wd_bf[a][:, :, :, i0 : i0 + raw.shape[1]].rearrange("p t m i -> p m i t"), src)
+        def cast_wd(a, copy):
+            for raw, c0 in wd_parts[a]:
+                dst = wd_bf[a][:, :, c0 // 4 : (c0 + raw.shape[2]) // 4, :]
+                copy(dst.rearrange("p t m i -> p m i t"), raw[:].rearrange("p i (m t) -> p m i t", t=4))
 
         def quant_wd(a):
             wd_codes[a] = kept([P, H], U32, f"wd_codes{a}")
@@ -163,7 +175,7 @@ def tile_list_momentum_block_steps_kernel(
                     nc.tensor.matmul_mx(
                         out=c_acc[b][t][:],
                         lhsT=wc_codes[m][:, a % 2, P * t : P * (t + 1)].bitcast(FP4X4),
-                        lhsT_scale=planes[0][:, a, HALF + P * t : HALF + P * (t + 1)],
+                        lhsT_scale=wc_planes[m][:, a % 2, P * t : P * (t + 1)],
                         rhs=rhs,
                         rhs_scale=rhs_scale,
                         start=(a == 0),
@@ -171,39 +183,46 @@ def tile_list_momentum_block_steps_kernel(
                     )
 
         order_wc(0, kept([P, 2, H], U16, "wc_codes0"))
-        gather_words(0, 0, placed([P, HALF], U32, "got_first", 41984))
+        gather_words(0, 0, placed([P, HALF], U32, "got00", GOT + 5120))
         part_words(0, 0)
         c_passes(0, 0)
-        gather_words(0, 1, placed([P, HALF], U32, "got0", 43008))
-        order_wc(1, placed([P, 2, H], U16, "wc_codes1", 40960))
+        gather_words(0, 1, placed([P, HALF], U32, "got01", GOT + 4096))
+        order_wc(1, placed([P, 2, H], U16, "wc_codes1", GOT + 6144))
+        for a in (1, 2):
+            wd_parts[a] = [load_wd(a, placed([P, 4, H], F32, f"wd{a}", LATE + 8192 * (a - 1)), 0)]
+        wd_parts[3] = [
+            load_wd(3, placed([P, 4, H // 2], F32, f"wd3_{half}", LAST + 4096 * half), H // 2 * half) for half in range(2)
+        ]
         part_words(0, 1)
         c_passes(0, 1)
-        for half in range(2):
-            cast_wd(0, wd0_raw[half], 2 * half, nc.scalar.copy)
-        gather_words(1, 0, kept([P, HALF], U32, "got1"))
-        gather_words(1, 1, placed([P, HALF], U32, "got0", 43008))
-        part_words(1, 0)
-        part_words(1, 1)
-        c_passes(1, 0)
-        c_passes(1, 1)
+        cast_wd(0, nc.scalar.copy)
+        got1 = placed([P, 2, HALF], U32, "got1", GOT + 2048)
+        for b in range(2):
+            gather_words(1, b, got1[:, b])
+        for b in range(2):
+            part_words(1, b)
+            c_passes(1, b)
 
-        wos = kept([P, N], U8, "tab_words0")
+        wo_codes = placed([P, N], U32, "wo_codes", TAB1 + 7168)
+        nc.sync.dma_start(wo_codes[:].bitcast(I32), wo_words[0].rearrange("p e i -> p (e i)").bitcast(I32))
+        wos = placed([P, N], U8, "wos", TAB1 + 6144)
         nc.vector.memset(wos[:].bitcast(I32), 0)
         for r in range(4):
             nc.sync.dma_start(wos[r:P:32, :].bitcast(I32), wo_scales[0, r:16:4, :].bitcast(I32))
-        rate_sb = kept([P, NT], F32, "got1")
+        rate_sb = placed([P, NT], F32, "rate_sb", TAB1 + 6912)
         with nc.allow_non_contiguous_dma(reason="one rate for each output row"):
             nc.sync.dma_start(rate_sb[:], rate.rearrange("(u p) -> p u", p=P))
 
         quant_wd(0)
         for a in range(1, PASSES):
-            cast_wd(a, wd_raw[a], 0, nc.vector.tensor_copy)
+            cast_wd(a, nc.vector.tensor_copy)
             quant_wd(a)
 
-        sq = [kept([P, 4, HALF], F32, f"sq{b}") for b in range(2)]
+        sq = {}
         damp = [kept([P, PAIR // RUN, 4, RUN], F32, f"damp{g}") for g in range(S // PAIR)]
 
         def squares(b):
+            sq[b] = placed([P, 4, HALF], F32, f"sq{b}", 8192 * b)
             for t in range(4):
                 nc.scalar.activation(sq[b][:, t, :], c_acc[b][t][:], ACT.Square)
 
@@ -301,41 +320,41 @@ def tile_list_momentum_block_steps_kernel(
                 nc.scalar.activation(res[:, e, :], acc[:, e, :], ACT.Copy, scale=rate_sb[:, u0 + e : u0 + e + 1])
             store(res, u0, c0)
 
-        for i in range(4):
-            for a in (0, 1):
-                d_pass(a, i, i)
-        for a in (2, 3):
+        for a in (0, 1):
             for i in range(4):
                 d_pass(a, i, i)
-        d_chunk(4)
+        for a in (0, 1):
+            d_pass(a, 4, 4)
+        for a in (2, 3):
+            for i in range(5):
+                d_pass(a, i, i)
+        d_chunk(5)
         for i in range(3):
             damp_chunk(i)
         quant_h(0, 2)
         pair0 = y_cols(0, PAIR, (0, 1, 2))
-        empty_on_scalar(*pair0[0])
-        d_chunk(5)
+        for part in pair0:
+            empty_on_scalar(*part)
+        d_chunk(6)
         damp_chunk(3)
         damp_chunk(4)
         quant_h(2, 2)
-        empty_on_vector(*pair0[1])
         pair1 = y_cols(PAIR, PAIR, (3, 4, 0))
-        empty_on_scalar(*pair1[0])
-        d_chunk(6)
         damp_chunk(5)
-        quant_h(4, 2)
-        empty_on_vector(*pair0[2])
         damp_chunk(6)
+        quant_h(4, 2)
         quant_h(6, 1)
-        empty_on_scalar(*pair1[1])
         pair2 = y_cols(2 * PAIR, PAIR, (1, 2, 5))
-        empty_on_vector(*pair1[2])
+        empty_on_scalar(*pair1[0])
+        empty_on_vector(*pair1[1])
+        empty_on_scalar(*pair1[2])
         d_chunk(7)
-        empty_on_scalar(*pair2[0])
-        empty_on_scalar(*pair2[1])
+        empty_on_vector(*pair2[0])
+        empty_on_vector(*pair2[1])
+        empty_on_scalar(*pair2[2])
         last_but_one = y_cols(6 * CHUNK, CHUNK, (6, 3))
         damp_chunk(7)
         quant_h(7, 1)
-        empty_on_vector(*pair2[2])
         empty_on_scalar(*last_but_one[0])
         last = y_cols(7 * CHUNK, CHUNK, (4, 0))
         empty_on_vector(*last_but_one[1])

@@ -25,8 +25,8 @@ NT = N // P
 ROW = HALF + H + HALF
 TAB1 = 10240
 GOT = TAB1 + 10240
-LATE = GOT + 8192
-LAST = LATE + 16384
+LATE = GOT + 10240
+LAST = LATE + 20480
 RUN = 2
 
 
@@ -102,7 +102,7 @@ def tile_list_momentum_block_steps_kernel(
         wd_parts = {0: [load_wd(0, kept([P, 4, H // 2], F32, "wd0_left"), 0)]}
 
         stage = placed([P, ROW], U8, "stage", LAST + 3328)
-        got_a = placed([P, HALF], U8, "got_a", TAB1)
+        got_a = placed([P, HALF], U8, "got_a", TAB1 - 256)
         nc.vector.tensor_copy(got_a[:], tab_scale[:].indirect(offsets[:, 0:32]))
         nc.vector.tensor_copy(
             stage[:, HALF : HALF + H].rearrange("p (t c i) -> p c t i", t=4, i=16),
@@ -110,12 +110,7 @@ def tile_list_momentum_block_steps_kernel(
         )
         nc.vector.tensor_copy(stage[0:64, 0:HALF].bitcast(I32), got_a[0:64, :].bitcast(I32))
         move_rows(first_planes, stage[:, 0 : HALF + H], 0, (nc.sync, nc.scalar))
-        tab_words.append(load_tab(1, placed([P, T], U32, "tab_words1", TAB1 + 256)))
-        got_b = placed([P, HALF], U8, "got_b", TAB1 - 256)
-        nc.vector.tensor_copy(got_b[:], tab_scale[:].indirect(offsets[:, 32:64]))
-        move_rows(second_planes, got_b, 0, (nc.sync, nc.sync))
-        nc.vector.tensor_copy(stage[0:64, HALF + H : ROW].bitcast(I32), got_b[0:64, :].bitcast(I32))
-        move_rows(late_planes, stage, 1, (nc.sync, nc.sync))
+        tab_words.append(load_tab(1, placed([P, T], U32, "tab_words1", TAB1)))
         wd_parts[0].append(load_wd(0, placed([P, 4, H // 2], F32, "wd0_right", TAB1 - 4096), H // 2))
 
         table_planes = [
@@ -152,8 +147,8 @@ def tile_list_momentum_block_steps_kernel(
         wd_bf = [kept([P, 4, P, 4], BF16, f"wd_bf{a}") for a in range(PASSES)]
         wd_codes, wd_scale = {}, {}
 
-        def cast_wd(a, copy):
-            for raw, c0 in wd_parts[a]:
+        def cast_wd(a, copy, parts):
+            for raw, c0 in parts:
                 dst = wd_bf[a][:, :, c0 // 4 : (c0 + raw.shape[2]) // 4, :]
                 copy(dst.rearrange("p t m i -> p m i t"), raw[:].rearrange("p i (m t) -> p m i t", t=4))
 
@@ -183,23 +178,29 @@ def tile_list_momentum_block_steps_kernel(
                     )
 
         order_wc(0, kept([P, 2, H], U16, "wc_codes0"))
-        gather_words(0, 0, placed([P, HALF], U32, "got00", GOT + 5120))
+        gather_words(0, 0, placed([P, HALF], U32, "got00", GOT + 4096))
         part_words(0, 0)
         c_passes(0, 0)
-        gather_words(0, 1, placed([P, HALF], U32, "got01", GOT + 4096))
-        order_wc(1, placed([P, 2, H], U16, "wc_codes1", GOT + 6144))
-        for a in (1, 2):
-            wd_parts[a] = [load_wd(a, placed([P, 4, H], F32, f"wd{a}", LATE + 8192 * (a - 1)), 0)]
+        got_b = placed([P, HALF], U8, "got_b", GOT + 5120)
+        nc.vector.tensor_copy(got_b[:], tab_scale[:].indirect(offsets[:, 32:64]))
+        move_rows(second_planes, got_b, 0, (nc.sync, nc.sync))
+        gather_words(0, 1, placed([P, HALF], U32, "got01", GOT + 3072))
+        nc.vector.tensor_copy(stage[0:64, HALF + H : ROW].bitcast(I32), got_b[0:64, :].bitcast(I32))
+        move_rows(late_planes, stage, 1, (nc.sync, nc.sync))
+        order_wc(1, placed([P, 2, H], U16, "wc_codes1", GOT + 5632))
+        wd_parts[1] = [load_wd(1, placed([P, 4, H // 2], F32, "wd1_left", LATE + 4096), 0)]
+        wd_mid = placed([P, 6 * H], F32, "wd_mid", LATE + 8192)
+        wd_parts[1].append(load_wd(1, wd_mid[:, 0 : 2 * H].rearrange("p (i r) -> p i r", i=4), H // 2))
+        wd_parts[2] = [load_wd(2, wd_mid[:, 2 * H : 6 * H].rearrange("p (i r) -> p i r", i=4), 0)]
         wd_parts[3] = [
             load_wd(3, placed([P, 4, H // 2], F32, f"wd3_{half}", LAST + 4096 * half), H // 2 * half) for half in range(2)
         ]
         part_words(0, 1)
         c_passes(0, 1)
-        cast_wd(0, nc.scalar.copy)
-        got1 = placed([P, 2, HALF], U32, "got1", GOT + 2048)
+        cast_wd(0, nc.scalar.copy, wd_parts[0])
+        cast_wd(1, nc.scalar.copy, wd_parts[1][:1])
         for b in range(2):
-            gather_words(1, b, got1[:, b])
-        for b in range(2):
+            gather_words(1, b, kept([P, HALF], U32, "got1"))
             part_words(1, b)
             c_passes(1, b)
 
@@ -214,15 +215,17 @@ def tile_list_momentum_block_steps_kernel(
             nc.sync.dma_start(rate_sb[:], rate.rearrange("(u p) -> p u", p=P))
 
         quant_wd(0)
-        for a in range(1, PASSES):
-            cast_wd(a, nc.vector.tensor_copy)
+        cast_wd(1, nc.vector.tensor_copy, wd_parts[1][1:])
+        quant_wd(1)
+        for a in range(2, PASSES):
+            cast_wd(a, nc.vector.tensor_copy, wd_parts[a])
             quant_wd(a)
 
         sq = {}
         damp = [kept([P, PAIR // RUN, 4, RUN], F32, f"damp{g}") for g in range(S // PAIR)]
 
         def squares(b):
-            sq[b] = placed([P, 4, HALF], F32, f"sq{b}", 8192 * b)
+            sq[b] = placed([P, 4, HALF], F32, f"sq{b}", (LATE - 2048, 0)[b])
             for t in range(4):
                 nc.scalar.activation(sq[b][:, t, :], c_acc[b][t][:], ACT.Square)
 

@@ -23,11 +23,14 @@ CHUNK = 128
 PAIR = 256
 NT = N // P
 ROW = HALF + H + HALF
-TAB1 = 10240
-GOT = TAB1 + 10240
-LATE = GOT + 10240
-LAST = LATE + 20480
+QUARTER = 256
 RUN = 2
+EARLY = 5
+GOT_A = 8192
+GOT_Q = 12288
+SCALES = 24576
+WD = SCALES + 1024
+GOT_V = 18432
 
 
 def tile_list_momentum_block_steps_kernel(
@@ -52,180 +55,162 @@ def tile_list_momentum_block_steps_kernel(
             return tile.rearrange("p a e -> p (a e)").bitcast(I32).rearrange("p (a e) -> p a e", a=tile.shape[1])
 
         offsets = keep.tile([P, S // 16], U16, name="offsets")
-        tab_scale = kept([P, T], U8, "tab_scale")
+        tab_scale = placed([P, T], U8, "tab_scale", SCALES)
         wcs_raw = kept([P, H], U8, "wcs_raw")
-        wc_raw = [kept([P, 2, H], U16, "wc_raw0"), placed([P, 2, H], U16, "wc_raw1", LATE + 7168)]
-        first_planes = kept([P, 2, HALF + H], U8, "first_planes")
-        second_planes = kept([P, 2, HALF], U8, "second_planes")
-        late_planes = kept([P, 2, ROW], U8, "late_planes")
+        first_planes = kept([P, PASSES, HALF + H], U8, "first_planes")
+        second_planes = kept([P, PASSES, HALF], U8, "second_planes")
         warm = keep.tile([P, 2], F32, name="warm")
 
         nc.vector.memset(warm[:, 0:1], 1.0)
         nc.scalar.activation(warm[:, 1:2], warm[:, 0:1], ACT.Abs_reciprocal_sqrt, bias=1.0)
-        nc.vector.memset(tab_scale[64:128, :].bitcast(I32), 0)
         nc.vector.memset(wcs_raw[64:128, :].bitcast(I32), 0)
-        for plane in (first_planes, second_planes, late_planes):
+        nc.vector.memset(tab_scale[64:128, :].bitcast(I32), 0)
+        for plane in (first_planes, second_planes):
             nc.vector.memset(plane[:].rearrange("p a e -> p (a e)").bitcast(I32), 0)
 
         nc.sync.dma_start(offsets[:], offs)
-        for m in range(2):
-            nc.sync.dma_start(
-                wcs_raw[32 * m : 32 * (m + 1), :].bitcast(I32), wc_scales.bitcast(I32)[2 * m : 2 * m + 2].rearrange("h q e -> q h e")
-            )
-        for m in range(2):
-            nc.sync.dma_start(
-                tab_scale[32 * m : 32 * (m + 1), :].bitcast(I32),
-                tab[m, 512 * T :].rearrange("(h q t) -> q h t", h=2, q=16).bitcast(I32),
-            )
+        for a in range(PASSES):
+            rows = tab[a // 2, 512 * T :].rearrange("(h q t) -> h q t", h=2, q=16)[a % 2]
+            nc.sync.dma_start(tab_scale[a:64:4, :].bitcast(I32), rows.bitcast(I32))
+        nc.sync.dma_start(wcs_raw[0:64, :].bitcast(I32), wc_scales.bitcast(I32).rearrange("a q e -> q a e"))
 
-        def load_wc(m):
-            nc.sync.dma_start(words(wc_raw[m][:]), wc_words.bitcast(I32)[2 * m : 2 * m + 2].rearrange("a p e -> p a e"))
+        def load_wc(m, raw):
+            nc.sync.dma_start(words(raw[:]), wc_words.bitcast(I32)[2 * m : 2 * m + 2].rearrange("a p e -> p a e"))
+            return raw
 
         def load_tab(m, tile):
             nc.sync.dma_start(tile[:].bitcast(I32), tab[m, 0 : 512 * T].rearrange("(p w) -> p w", p=P).bitcast(I32))
             return tile
 
-        def load_wd(a, raw, c0):
-            rows = wd[512 * a : 512 * (a + 1), :].rearrange("(p i) r -> p i r", i=4)
-            nc.sync.dma_start(raw[:], rows[:, :, c0 : c0 + raw.shape[2]])
-            return raw, c0
-
-        def move_rows(plane, rows, m, queues):
+        def move_rows(plane, rows, queues):
             for q in (0, 2, 1, 3):
                 queues[q // 2].dma_start(
-                    words(plane[32 * q : 32 * q + 4]), rows[32 * m + 8 * q : 32 * m + 8 * (q + 1), :].bitcast(I32)
+                    words(plane[32 * q : 32 * q + 4]), rows[16 * q : 16 * (q + 1), :].bitcast(I32)
                 )
 
-        load_wc(0)
         tab_words = [load_tab(0, kept([P, T], U32, "tab_words0"))]
-        load_wc(1)
-        wd_parts = {0: [load_wd(0, kept([P, 4, H // 2], F32, "wd0_left"), 0)]}
+        wc_raw = [load_wc(0, kept([P, 2, H], U16, "wc_raw0"))]
 
-        stage = placed([P, ROW], U8, "stage", LAST + 3328)
-        got_a = placed([P, HALF], U8, "got_a", TAB1 - 256)
+        stage = kept([P, HALF + H], U8, "stage")
+        got_a = placed([P, HALF], U8, "got_a", GOT_A)
         nc.vector.tensor_copy(got_a[:], tab_scale[:].indirect(offsets[:, 0:32]))
         nc.vector.tensor_copy(
             stage[:, HALF : HALF + H].rearrange("p (t c i) -> p c t i", t=4, i=16),
             wcs_raw[:].rearrange("p (c i t) -> p c t i", t=4, i=16),
         )
         nc.vector.tensor_copy(stage[0:64, 0:HALF].bitcast(I32), got_a[0:64, :].bitcast(I32))
-        move_rows(first_planes, stage[:, 0 : HALF + H], 0, (nc.sync, nc.scalar))
-        tab_words.append(load_tab(1, placed([P, T], U32, "tab_words1", TAB1)))
-        wd_parts[0].append(load_wd(0, placed([P, 4, H // 2], F32, "wd0_right", TAB1 - 4096), H // 2))
+        move_rows(first_planes, stage, (nc.sync, nc.scalar))
+        tab_words.append(load_tab(1, placed([P, T], U32, "tab_words1", GOT_A + 256 - 4 * T)))
 
-        table_planes = [
-            [first_planes[:, :, 0:HALF], second_planes],
-            [late_planes[:, :, 0:HALF], late_planes[:, :, HALF + H : ROW]],
-        ]
-        wc_planes = [plane[:, :, HALF : HALF + H] for plane in (first_planes, late_planes)]
-        wc_codes, got, v_codes = {}, {}, {}
+        table_planes = [first_planes[:, :, 0:HALF], second_planes]
+        wc_planes = first_planes[:, :, HALF : HALF + H]
+        wc_first = placed([P, 2 * H], U16, "wc_first", GOT_A + 256)
+        wc_codes = [wc_first[:, H * a : H * (a + 1)] for a in range(2)]
+        wc_codes.extend(kept([P, H], U16, f"wc_codes{a}") for a in range(2, PASSES))
+        v_codes = [[], []]
 
-        def order_wc(m, codes):
-            wc_codes[m] = codes
-            nc.vector.tensor_copy(
-                codes[:].rearrange("p a (t c i) -> p a c t i", t=4, i=8),
-                wc_raw[m][:].rearrange("p a (c i t) -> p a c t i", t=4, i=8),
+        def order_wc(a):
+            nc.scalar.copy(
+                wc_codes[a][:].rearrange("p (t c i) -> p c t i", t=4, i=8),
+                wc_raw[a // 2][:, a % 2, :].rearrange("p (c i t) -> p c t i", t=4, i=8),
             )
 
-        def gather_words(m, b, tile):
-            got[(m, b)] = tile
-            nc.vector.tensor_copy(tile[:], tab_words[m][:].indirect(offsets[:, 32 * b : 32 * (b + 1)]))
+        def gather_words(m, c0, tile):
+            width = tile.shape[1]
+            nc.vector.tensor_copy(tile[:], tab_words[m][:].indirect(offsets[:, c0 // 16 : (c0 + width) // 16]))
+            return m, c0, tile
 
-        def part_words(m, b):
-            codes = kept([P, 2, HALF], U16, f"v_codes{m}{b}")
+        def part_words(m, c0, tile):
+            shape, name = [P, 2, tile.shape[1]], f"v_codes{m}_{c0}"
+            codes = placed(shape, U16, name, GOT_V - 2048) if (m, c0) == (1, 0) else kept(shape, U16, name)
+            v_codes[m].append((c0, codes))
             nc.vector.tensor_copy(
                 codes[:].rearrange("p h (c i) -> p c h i", i=8),
-                got[(m, b)][:].bitcast(U16).rearrange("p (c i h) -> p c h i", i=8, h=2),
+                tile[:].bitcast(U16).rearrange("p (c i h) -> p c h i", i=8, h=2),
             )
-            v_codes[(m, b)] = codes
 
         def v_operand(a, c0, width):
             m, h = divmod(a, 2)
             b, o = divmod(c0, HALF)
-            return v_codes[(m, b)][:, h, o : o + width].bitcast(FP4X4), table_planes[m][b][:, h, o : o + width]
-
-        wd_bf = [kept([P, 4, P, 4], BF16, f"wd_bf{a}") for a in range(PASSES)]
-        wd_codes, wd_scale = {}, {}
-
-        def cast_wd(a, copy, parts):
-            for raw, c0 in parts:
-                dst = wd_bf[a][:, :, c0 // 4 : (c0 + raw.shape[2]) // 4, :]
-                copy(dst.rearrange("p t m i -> p m i t"), raw[:].rearrange("p i (m t) -> p m i t", t=4))
-
-        def quant_wd(a):
-            wd_codes[a] = kept([P, H], U32, f"wd_codes{a}")
-            wd_scale[a] = kept([P, H], U8, f"wd_scale{a}")
-            nc.vector.quantize_mx(
-                out=wd_codes[a][:].bitcast(FP8X4),
-                scales=wd_scale[a][:],
-                in_=wd_bf[a][:].rearrange("p t m i -> p (t m i)"),
-            )
+            start, codes = [piece for piece in v_codes[m] if piece[0] <= c0][-1]
+            return codes[:, h, c0 - start : c0 - start + width].bitcast(FP4X4), table_planes[b][:, a, o : o + width]
 
         c_acc = [[bank([P, HALF], 4 * b + t) for t in range(4)] for b in range(2)]
 
-        def c_passes(m, b):
-            for t in range(4):
-                for a in (2 * m, 2 * m + 1):
-                    rhs, rhs_scale = v_operand(a, HALF * b, HALF)
+        def c_passes(m, c0, width):
+            b, o = divmod(c0, HALF)
+            for a in (2 * m, 2 * m + 1):
+                for t in range(4):
+                    rhs, rhs_scale = v_operand(a, c0, width)
                     nc.tensor.matmul_mx(
-                        out=c_acc[b][t][:],
-                        lhsT=wc_codes[m][:, a % 2, P * t : P * (t + 1)].bitcast(FP4X4),
-                        lhsT_scale=wc_planes[m][:, a % 2, P * t : P * (t + 1)],
+                        out=c_acc[b][t][:, o : o + width],
+                        lhsT=wc_codes[a][:, P * t : P * (t + 1)].bitcast(FP4X4),
+                        lhsT_scale=wc_planes[:, a, P * t : P * (t + 1)],
                         rhs=rhs,
                         rhs_scale=rhs_scale,
-                        start=(a == 0),
+                        start=(a == 0 and o == 0),
                         stop=(a == PASSES - 1),
                     )
 
-        order_wc(0, kept([P, 2, H], U16, "wc_codes0"))
-        gather_words(0, 0, placed([P, HALF], U32, "got00", GOT + 4096))
-        part_words(0, 0)
-        c_passes(0, 0)
-        got_b = placed([P, HALF], U8, "got_b", GOT + 5120)
+        order_wc(0)
+        order_wc(1)
+        first = gather_words(0, 0, placed([P, QUARTER], U32, "got_q0", GOT_V))
+        second = gather_words(0, QUARTER, placed([P, QUARTER], U32, "got_q1", GOT_Q))
+        part_words(*first)
+        c_passes(0, 0, QUARTER)
+        part_words(*second)
+        c_passes(0, QUARTER, QUARTER)
+        got_b = placed([P, HALF], U8, "got_b", GOT_V - 256)
         nc.vector.tensor_copy(got_b[:], tab_scale[:].indirect(offsets[:, 32:64]))
-        move_rows(second_planes, got_b, 0, (nc.sync, nc.sync))
-        gather_words(0, 1, placed([P, HALF], U32, "got01", GOT + 3072))
-        nc.vector.tensor_copy(stage[0:64, HALF + H : ROW].bitcast(I32), got_b[0:64, :].bitcast(I32))
-        move_rows(late_planes, stage, 1, (nc.sync, nc.sync))
-        order_wc(1, placed([P, 2, H], U16, "wc_codes1", GOT + 5632))
-        wd_parts[1] = [load_wd(1, placed([P, 4, H // 2], F32, "wd1_left", LATE + 4096), 0)]
-        wd_mid = placed([P, 6 * H], F32, "wd_mid", LATE + 8192)
-        wd_parts[1].append(load_wd(1, wd_mid[:, 0 : 2 * H].rearrange("p (i r) -> p i r", i=4), H // 2))
-        wd_parts[2] = [load_wd(2, wd_mid[:, 2 * H : 6 * H].rearrange("p (i r) -> p i r", i=4), 0)]
-        wd_parts[3] = [
-            load_wd(3, placed([P, 4, H // 2], F32, f"wd3_{half}", LAST + 4096 * half), H // 2 * half) for half in range(2)
-        ]
-        part_words(0, 1)
-        c_passes(0, 1)
-        cast_wd(0, nc.scalar.copy, wd_parts[0])
-        cast_wd(1, nc.scalar.copy, wd_parts[1][:1])
-        for b in range(2):
-            gather_words(1, b, kept([P, HALF], U32, "got1"))
-            part_words(1, b)
-            c_passes(1, b)
+        move_rows(second_planes, got_b, (nc.sync, nc.scalar))
+        wc_raw.append(load_wc(1, placed([P, 2, H], U16, "wc_raw1", SCALES - 1024)))
+        third = gather_words(0, HALF, placed([P, HALF], U32, "got_b0", GOT_V + 512))
 
-        wo_codes = placed([P, N], U32, "wo_codes", TAB1 + 7168)
+        wd_all = placed([P, PASSES * 4 * H], F32, "wd_all", WD)
+        wd_raw = [wd_all[:, 4 * H * a : 4 * H * (a + 1)] for a in range(PASSES)]
+        for a in range(PASSES):
+            nc.sync.dma_start(wd_raw[a], wd[512 * a : 512 * (a + 1), :].rearrange("(p i) r -> p (i r)", i=4))
+
+        part_words(*third)
+        c_passes(0, HALF, HALF)
+        order_wc(2)
+        order_wc(3)
+        late = [gather_words(1, HALF * b, placed([P, HALF], U32, f"got_1{b}", GOT_V + 2048 * (1 - b))) for b in range(2)]
+        for b in range(2):
+            part_words(*late[b])
+            c_passes(1, HALF * b, HALF)
+
+        wo_codes = placed([P, N], U32, "wo_codes", 0)
         nc.sync.dma_start(wo_codes[:].bitcast(I32), wo_words[0].rearrange("p e i -> p (e i)").bitcast(I32))
-        wos = placed([P, N], U8, "wos", TAB1 + 6144)
+        wos = placed([P, N], U8, "wos", 4096)
         nc.vector.memset(wos[:].bitcast(I32), 0)
         for r in range(4):
             nc.sync.dma_start(wos[r:P:32, :].bitcast(I32), wo_scales[0, r:16:4, :].bitcast(I32))
-        rate_sb = placed([P, NT], F32, "rate_sb", TAB1 + 6912)
+        rate_sb = placed([P, NT], F32, "rate_sb", 5120)
         with nc.allow_non_contiguous_dma(reason="one rate for each output row"):
             nc.sync.dma_start(rate_sb[:], rate.rearrange("(u p) -> p u", p=P))
 
-        quant_wd(0)
-        cast_wd(1, nc.vector.tensor_copy, wd_parts[1][1:])
-        quant_wd(1)
-        for a in range(2, PASSES):
-            cast_wd(a, nc.vector.tensor_copy, wd_parts[a])
-            quant_wd(a)
+        wd_bf = [[kept([P, 2, P, 4], BF16, f"wd_bf{a}{s}") for s in range(2)] for a in range(PASSES)]
+        wd_codes = [kept([P, H], U32, f"wd_codes{a}") for a in range(PASSES)]
+        wd_scale = [kept([P, H], U8, f"wd_scale{a}") for a in range(PASSES)]
 
-        sq = {}
+        def cast_wd(a, s, copy):
+            copy(
+                wd_bf[a][s][:].rearrange("p t m i -> p m i t"),
+                wd_raw[a].rearrange("p (i m t) -> p m i t", i=4, t=4)[:, :, :, 2 * s : 2 * s + 2],
+            )
+
+        def quant_wd(a, s):
+            nc.vector.quantize_mx(
+                out=wd_codes[a][:, 2 * P * s : 2 * P * (s + 1)].bitcast(FP8X4),
+                scales=wd_scale[a][:, 2 * P * s : 2 * P * (s + 1)],
+                in_=wd_bf[a][s][:].rearrange("p t m i -> p (t m i)"),
+            )
+
+        sq = [kept([P, 4, HALF], F32, f"sq{b}") for b in range(2)]
         damp = [kept([P, PAIR // RUN, 4, RUN], F32, f"damp{g}") for g in range(S // PAIR)]
 
         def squares(b):
-            sq[b] = placed([P, 4, HALF], F32, f"sq{b}", (LATE - 2048, 0)[b])
             for t in range(4):
                 nc.scalar.activation(sq[b][:, t, :], c_acc[b][t][:], ACT.Square)
 
@@ -239,16 +224,24 @@ def tile_list_momentum_block_steps_kernel(
             )
 
         squares(0)
-        rsqrt(0)
         squares(1)
+        rsqrt(0)
+        for a in range(PASSES):
+            cast_wd(a, 0, nc.vector.tensor_copy)
+            cast_wd(a, 1, nc.vector.tensor_copy)
+            quant_wd(a, 0)
+            quant_wd(a, 1)
         for g in range(1, 4):
             rsqrt(g)
 
         d_acc = {}
 
-        def d_pass(a, i, b, first=0, last=PASSES - 1):
-            if a == first:
-                d_acc[i] = bank([P, 4, CHUNK], b)
+        def d_order(i):
+            return list(range(PASSES)) if i < EARLY else list(reversed(range(PASSES)))
+
+        def d_pass(a, i):
+            if a == d_order(i)[0]:
+                d_acc[i] = bank([P, 4, CHUNK], i)
             rhs, rhs_scale = v_operand(a, CHUNK * i, CHUNK)
             for t in range(4):
                 nc.tensor.matmul_mx(
@@ -257,17 +250,13 @@ def tile_list_momentum_block_steps_kernel(
                     lhsT_scale=wd_scale[a][:, P * t : P * (t + 1)],
                     rhs=rhs,
                     rhs_scale=rhs_scale,
-                    start=(a == first and t == 0),
-                    stop=(a == last and t == 3),
+                    start=(a == d_order(i)[0] and t == 0),
+                    stop=(a == d_order(i)[-1] and t == 3),
                 )
 
-        def d_chunk(i):
-            for a in reversed(range(PASSES)):
-                d_pass(a, i, i, PASSES - 1, 0)
-
         h_bf = [kept([P, 2, CHUNK, 4], BF16, f"h_bf{g}") for g in range(S // PAIR)]
-        h_codes = [kept([P, HALF], U32, f"h_codes{b}") for b in range(2)]
-        h_scale = [kept([P, HALF], U8, f"h_scale{b}") for b in range(2)]
+        h_codes = [kept([P, PAIR], U32, f"h_codes{g}") for g in range(S // PAIR)]
+        h_scale = [kept([P, PAIR], U8, f"h_scale{g}") for g in range(S // PAIR)]
 
         def damp_chunk(i):
             g, e = divmod(i, 2)
@@ -279,33 +268,26 @@ def tile_list_momentum_block_steps_kernel(
                 MULT,
             )
 
-        def quant_h(i, chunks):
-            g, e = divmod(i, 2)
-            b, o = divmod(CHUNK * i, HALF)
+        def quant_h(g):
             nc.vector.quantize_mx(
-                out=h_codes[b][:, o : o + CHUNK * chunks].bitcast(FP8X4),
-                scales=h_scale[b][:, o : o + CHUNK * chunks],
-                in_=h_bf[g][:, e : e + chunks].rearrange("p c n t -> p (c n t)"),
+                out=h_codes[g][:].bitcast(FP8X4),
+                scales=h_scale[g][:],
+                in_=h_bf[g][:].rearrange("p c n t -> p (c n t)"),
             )
 
-        def y_pass(acc, u, c0, width):
-            b, o = divmod(c0, HALF)
-            nc.tensor.matmul_mx(
-                out=acc,
-                lhsT=wo_codes[:, P * u : P * (u + 1)].bitcast(FP8X4),
-                lhsT_scale=wos[:, P * u : P * (u + 1)],
-                rhs=h_codes[b][:, o : o + width].bitcast(FP8X4),
-                rhs_scale=h_scale[b][:, o : o + width],
-                start=True,
-                stop=True,
-            )
-
-        def y_cols(c0, width, banks):
-            per_bank = NT // len(banks)
-            accs = [bank([P, per_bank, width], b) for b in banks]
+        def y_pair(g, banks):
+            accs = [bank([P, 2, PAIR], b) for b in banks]
             for u in range(NT):
-                y_pass(accs[u // per_bank][:, u % per_bank, :], u, c0, width)
-            return [(acc, per_bank * bk, c0) for bk, acc in enumerate(accs)]
+                nc.tensor.matmul_mx(
+                    out=accs[u // 2][:, u % 2, :],
+                    lhsT=wo_codes[:, P * u : P * (u + 1)].bitcast(FP8X4),
+                    lhsT_scale=wos[:, P * u : P * (u + 1)],
+                    rhs=h_codes[g][:].bitcast(FP8X4),
+                    rhs_scale=h_scale[g][:],
+                    start=True,
+                    stop=True,
+                )
+            return [(acc, 2 * bk, PAIR * g) for bk, acc in enumerate(accs)]
 
         def store(res, u0, c0):
             rows, width = res.shape[1], res.shape[2]
@@ -323,43 +305,42 @@ def tile_list_momentum_block_steps_kernel(
                 nc.scalar.activation(res[:, e, :], acc[:, e, :], ACT.Copy, scale=rate_sb[:, u0 + e : u0 + e + 1])
             store(res, u0, c0)
 
+        def d_rest(i):
+            for a in d_order(i)[2 if i < EARLY else 0 :]:
+                d_pass(a, i)
+
         for a in (0, 1):
-            for i in range(4):
-                d_pass(a, i, i)
-        for a in (0, 1):
-            d_pass(a, 4, 4)
+            for i in range(EARLY):
+                d_pass(a, i)
         for a in (2, 3):
-            for i in range(5):
-                d_pass(a, i, i)
-        d_chunk(5)
-        for i in range(3):
-            damp_chunk(i)
-        quant_h(0, 2)
-        pair0 = y_cols(0, PAIR, (0, 1, 2))
-        for part in pair0:
+            for i in range(4):
+                d_pass(a, i)
+        d_rest(4)
+        damp_chunk(0)
+        damp_chunk(1)
+        quant_h(0)
+        for part in y_pair(0, (7, 0, 1)):
             empty_on_scalar(*part)
-        d_chunk(6)
-        damp_chunk(3)
-        damp_chunk(4)
-        quant_h(2, 2)
-        pair1 = y_cols(PAIR, PAIR, (3, 4, 0))
+        d_rest(5)
+        d_rest(6)
+        for i in (2, 3, 4):
+            damp_chunk(i)
+        quant_h(1)
+        pair1 = y_pair(1, (2, 3, 4))
         damp_chunk(5)
         damp_chunk(6)
-        quant_h(4, 2)
-        quant_h(6, 1)
-        pair2 = y_cols(2 * PAIR, PAIR, (1, 2, 5))
+        quant_h(2)
         empty_on_scalar(*pair1[0])
         empty_on_vector(*pair1[1])
-        empty_on_scalar(*pair1[2])
-        d_chunk(7)
-        empty_on_vector(*pair2[0])
-        empty_on_vector(*pair2[1])
-        empty_on_scalar(*pair2[2])
-        last_but_one = y_cols(6 * CHUNK, CHUNK, (6, 3))
+        empty_on_vector(*pair1[2])
+        d_rest(7)
+        pair2 = y_pair(2, (0, 1, 5))
         damp_chunk(7)
-        quant_h(7, 1)
-        empty_on_scalar(*last_but_one[0])
-        last = y_cols(7 * CHUNK, CHUNK, (4, 0))
-        empty_on_vector(*last_but_one[1])
-        empty_on_scalar(*last[0])
-        empty_on_vector(*last[1])
+        quant_h(3)
+        empty_on_scalar(*pair2[0])
+        empty_on_scalar(*pair2[1])
+        empty_on_vector(*pair2[2])
+        pair3 = y_pair(3, (6, 7, 2))
+        empty_on_vector(*pair3[0])
+        empty_on_scalar(*pair3[1])
+        empty_on_vector(*pair3[2])

@@ -135,7 +135,6 @@ def tile_list_momentum_block_steps_kernel(
             start, codes = [piece for piece in v_codes[m] if piece[0] <= c0][-1]
             return codes[:, h, c0 - start : c0 - start + width].bitcast(FP4X4), table_planes[b][:, a, o : o + width]
 
-        c_acc = [[bank([P, HALF], 4 * b + t) for t in range(4)] for b in range(2)]
 
         def c_passes(m, c0, width):
             b, o = divmod(c0, HALF)
@@ -152,6 +151,18 @@ def tile_list_momentum_block_steps_kernel(
                         stop=(a == PASSES - 1),
                     )
 
+        idle = bank([P, HALF], 7)
+        for w in range(4):
+            nc.tensor.matmul_mx(
+                out=idle[:],
+                lhsT=wc_raw[0][:, 0, 0:P].bitcast(FP4X4),
+                lhsT_scale=wcs_raw[:, 0:P],
+                rhs=wc_raw[0][:, 1, :].bitcast(FP4X4),
+                rhs_scale=wcs_raw[:],
+                start=True,
+                stop=True,
+            )
+        c_acc = [[bank([P, HALF], 4 * b + t) for t in range(4)] for b in range(2)]
         order_wc(0)
         order_wc(1)
         first = gather_words(0, 0, placed([P, QUARTER], U32, "got_q0", GOT_V))
@@ -175,9 +186,8 @@ def tile_list_momentum_block_steps_kernel(
         c_passes(0, HALF, HALF)
         order_wc(2)
         order_wc(3)
-        late = [gather_words(1, HALF * b, placed([P, HALF], U32, f"got_1{b}", GOT_V + 2048 * (1 - b))) for b in range(2)]
         for b in range(2):
-            part_words(*late[b])
+            part_words(*gather_words(1, HALF * b, placed([P, HALF], U32, f"got_1{b}", GOT_V + 2048)))
             c_passes(1, HALF * b, HALF)
 
         wo_codes = placed([P, N], U32, "wo_codes", 0)
@@ -223,12 +233,15 @@ def tile_list_momentum_block_steps_kernel(
                 bias=1.0,
             )
 
+        cast_wd(0, 0, nc.scalar.copy)
+        cast_wd(0, 1, nc.scalar.copy)
         squares(0)
         squares(1)
         rsqrt(0)
         for a in range(PASSES):
-            cast_wd(a, 0, nc.vector.tensor_copy)
-            cast_wd(a, 1, nc.vector.tensor_copy)
+            if a > 0:
+                cast_wd(a, 0, nc.vector.tensor_copy)
+                cast_wd(a, 1, nc.vector.tensor_copy)
             quant_wd(a, 0)
             quant_wd(a, 1)
         for g in range(1, 4):
@@ -268,41 +281,53 @@ def tile_list_momentum_block_steps_kernel(
                 MULT,
             )
 
-        def quant_h(g):
+        def quant_h(i, chunks):
+            g, e = divmod(i, 2)
             nc.vector.quantize_mx(
-                out=h_codes[g][:].bitcast(FP8X4),
-                scales=h_scale[g][:],
-                in_=h_bf[g][:].rearrange("p c n t -> p (c n t)"),
+                out=h_codes[g][:, CHUNK * e : CHUNK * (e + chunks)].bitcast(FP8X4),
+                scales=h_scale[g][:, CHUNK * e : CHUNK * (e + chunks)],
+                in_=h_bf[g][:, e : e + chunks].rearrange("p c n t -> p (c n t)"),
             )
 
-        def y_pair(g, banks):
-            accs = [bank([P, 2, PAIR], b) for b in banks]
+        def y_cols(i, chunks, banks):
+            g, e = divmod(i, 2)
+            per_bank = NT // len(banks)
+            cols = slice(CHUNK * e, CHUNK * (e + chunks))
+            accs = [bank([P, per_bank, CHUNK * chunks], b) for b in banks]
             for u in range(NT):
                 nc.tensor.matmul_mx(
-                    out=accs[u // 2][:, u % 2, :],
+                    out=accs[u // per_bank][:, u % per_bank, :],
                     lhsT=wo_codes[:, P * u : P * (u + 1)].bitcast(FP8X4),
                     lhsT_scale=wos[:, P * u : P * (u + 1)],
-                    rhs=h_codes[g][:].bitcast(FP8X4),
-                    rhs_scale=h_scale[g][:],
+                    rhs=h_codes[g][:, cols].bitcast(FP8X4),
+                    rhs_scale=h_scale[g][:, cols],
                     start=True,
                     stop=True,
                 )
-            return [(acc, 2 * bk, PAIR * g) for bk, acc in enumerate(accs)]
+            return [(acc, per_bank * bk) for bk, acc in enumerate(accs)]
+
+        made = {}
+
+        def result(u0, rows, c0, width):
+            made[(c0, u0)] = kept([P, rows, width], F32, f"res{c0}_{u0}")
+            return made[(c0, u0)]
 
         def store(res, u0, c0):
             rows, width = res.shape[1], res.shape[2]
             nc.sync.dma_start(out[P * u0 : P * (u0 + rows), c0 : c0 + width].rearrange("(e p) j -> p e j", p=P), res[:])
 
-        def empty_on_vector(acc, u0, c0):
-            res = kept(acc.shape, F32, f"res{c0}_{u0}")
+        def on_vector(res, acc, u0):
             rates = rate_sb[:, u0 : u0 + acc.shape[1]].unsqueeze(2).to_broadcast(acc.shape)
-            nc.vector.tensor_tensor(res[:], acc[:], rates, MULT)
-            store(res, u0, c0)
+            nc.vector.tensor_tensor(res, acc[:], rates, MULT)
 
-        def empty_on_scalar(acc, u0, c0):
-            res = kept(acc.shape, F32, f"res{c0}_{u0}")
+        def on_scalar(res, acc, u0):
             for e in range(acc.shape[1]):
                 nc.scalar.activation(res[:, e, :], acc[:, e, :], ACT.Copy, scale=rate_sb[:, u0 + e : u0 + e + 1])
+
+        def empty(engine, part, c0):
+            acc, u0 = part
+            res = result(u0, acc.shape[1], c0, acc.shape[2])
+            engine(res[:], acc, u0)
             store(res, u0, c0)
 
         def d_rest(i):
@@ -312,35 +337,45 @@ def tile_list_momentum_block_steps_kernel(
         for a in (0, 1):
             for i in range(EARLY):
                 d_pass(a, i)
-        for a in (2, 3):
-            for i in range(4):
-                d_pass(a, i)
+        for i in range(4):
+            d_pass(2, i)
+        for i in range(2):
+            d_pass(3, i)
         d_rest(4)
+        for a in d_order(5)[:2]:
+            d_pass(a, 5)
+        for i in range(2, 4):
+            d_pass(3, i)
         damp_chunk(0)
         damp_chunk(1)
-        quant_h(0)
-        for part in y_pair(0, (7, 0, 1)):
-            empty_on_scalar(*part)
-        d_rest(5)
+        quant_h(0, 2)
+        for part in y_cols(0, 2, (7, 0, 1)):
+            empty(on_scalar, part, 0)
+        for a in d_order(5)[2:]:
+            d_pass(a, 5)
         d_rest(6)
         for i in (2, 3, 4):
             damp_chunk(i)
-        quant_h(1)
-        pair1 = y_pair(1, (2, 3, 4))
+        quant_h(2, 2)
+        pair1 = y_cols(2, 2, (2, 3, 4))
         damp_chunk(5)
         damp_chunk(6)
-        quant_h(2)
-        empty_on_scalar(*pair1[0])
-        empty_on_vector(*pair1[1])
-        empty_on_vector(*pair1[2])
+        quant_h(4, 2)
+        quant_h(6, 1)
+        empty(on_scalar, pair1[0], PAIR)
+        empty(on_vector, pair1[1], PAIR)
+        empty(on_vector, pair1[2], PAIR)
         d_rest(7)
-        pair2 = y_pair(2, (0, 1, 5))
+        pair2 = y_cols(4, 2, (0, 1, 5))
         damp_chunk(7)
-        quant_h(3)
-        empty_on_scalar(*pair2[0])
-        empty_on_scalar(*pair2[1])
-        empty_on_vector(*pair2[2])
-        pair3 = y_pair(3, (6, 7, 2))
-        empty_on_vector(*pair3[0])
-        empty_on_scalar(*pair3[1])
-        empty_on_vector(*pair3[2])
+        quant_h(7, 1)
+        empty(on_scalar, pair2[0], 2 * PAIR)
+        empty(on_scalar, pair2[1], 2 * PAIR)
+        empty(on_vector, pair2[2], 2 * PAIR)
+        ends = [result(3 * k, 3, 3 * PAIR, PAIR) for k in range(2)]
+        for e, banks in enumerate(((6, 2), (3, 4))):
+            parts = y_cols(6 + e, 1, banks)
+            for k, engine in enumerate((on_scalar, on_vector)):
+                engine(ends[k][:, :, CHUNK * e : CHUNK * (e + 1)], *parts[k])
+        for k in range(2):
+            store(ends[k], 3 * k, 3 * PAIR)

@@ -25,12 +25,12 @@ NT = N // P
 ROW = HALF + H + HALF
 QUARTER = 256
 RUN = 2
-EARLY = 5
+EARLY = 6
 GOT_A = 8192
 GOT_Q = 12288
-SCALES = 24576
-WD = SCALES + 1024
-GOT_V = 18432
+SCALES = 15360
+WD = 18432
+GOT_V = WD + 32768 + 128
 
 
 def tile_list_momentum_block_steps_kernel(
@@ -57,22 +57,28 @@ def tile_list_momentum_block_steps_kernel(
         offsets = keep.tile([P, S // 16], U16, name="offsets")
         tab_scale = placed([P, T], U8, "tab_scale", SCALES)
         wcs_raw = kept([P, H], U8, "wcs_raw")
-        first_planes = kept([P, PASSES, HALF + H], U8, "first_planes")
-        second_planes = kept([P, PASSES, HALF], U8, "second_planes")
+        first_planes = kept([P, 2, HALF + H], U8, "first_planes")
+        second_planes = kept([P, 2, HALF], U8, "second_planes")
+        late_planes = kept([P, 2, ROW], U8, "late_planes")
         warm = keep.tile([P, 2], F32, name="warm")
 
         nc.vector.memset(warm[:, 0:1], 1.0)
         nc.scalar.activation(warm[:, 1:2], warm[:, 0:1], ACT.Abs_reciprocal_sqrt, bias=1.0)
         nc.vector.memset(wcs_raw[64:128, :].bitcast(I32), 0)
         nc.vector.memset(tab_scale[64:128, :].bitcast(I32), 0)
-        for plane in (first_planes, second_planes):
+        for plane in (first_planes, second_planes, late_planes):
             nc.vector.memset(plane[:].rearrange("p a e -> p (a e)").bitcast(I32), 0)
 
         nc.sync.dma_start(offsets[:], offs)
-        for a in range(PASSES):
-            rows = tab[a // 2, 512 * T :].rearrange("(h q t) -> h q t", h=2, q=16)[a % 2]
-            nc.sync.dma_start(tab_scale[a:64:4, :].bitcast(I32), rows.bitcast(I32))
-        nc.sync.dma_start(wcs_raw[0:64, :].bitcast(I32), wc_scales.bitcast(I32).rearrange("a q e -> q a e"))
+        for m in range(2):
+            nc.sync.dma_start(
+                tab_scale[32 * m : 32 * (m + 1), :].bitcast(I32),
+                tab[m, 512 * T :].rearrange("(h q t) -> q h t", h=2, q=16).bitcast(I32),
+            )
+        for m in range(2):
+            nc.sync.dma_start(
+                wcs_raw[32 * m : 32 * (m + 1), :].bitcast(I32), wc_scales.bitcast(I32)[2 * m : 2 * m + 2].rearrange("h q e -> q h e")
+            )
 
         def load_wc(m, raw):
             nc.sync.dma_start(words(raw[:]), wc_words.bitcast(I32)[2 * m : 2 * m + 2].rearrange("a p e -> p a e"))
@@ -82,16 +88,16 @@ def tile_list_momentum_block_steps_kernel(
             nc.sync.dma_start(tile[:].bitcast(I32), tab[m, 0 : 512 * T].rearrange("(p w) -> p w", p=P).bitcast(I32))
             return tile
 
-        def move_rows(plane, rows, queues):
+        def move_rows(plane, rows, m, queues):
             for q in (0, 2, 1, 3):
                 queues[q // 2].dma_start(
-                    words(plane[32 * q : 32 * q + 4]), rows[16 * q : 16 * (q + 1), :].bitcast(I32)
+                    words(plane[32 * q : 32 * q + 4]), rows[32 * m + 8 * q : 32 * m + 8 * (q + 1), :].bitcast(I32)
                 )
 
         tab_words = [load_tab(0, kept([P, T], U32, "tab_words0"))]
         wc_raw = [load_wc(0, kept([P, 2, H], U16, "wc_raw0"))]
 
-        stage = kept([P, HALF + H], U8, "stage")
+        stage = kept([P, ROW], U8, "stage")
         got_a = placed([P, HALF], U8, "got_a", GOT_A)
         nc.vector.tensor_copy(got_a[:], tab_scale[:].indirect(offsets[:, 0:32]))
         nc.vector.tensor_copy(
@@ -99,11 +105,14 @@ def tile_list_momentum_block_steps_kernel(
             wcs_raw[:].rearrange("p (c i t) -> p c t i", t=4, i=16),
         )
         nc.vector.tensor_copy(stage[0:64, 0:HALF].bitcast(I32), got_a[0:64, :].bitcast(I32))
-        move_rows(first_planes, stage, (nc.sync, nc.scalar))
+        move_rows(first_planes, stage[:, 0 : HALF + H], 0, (nc.sync, nc.sync))
         tab_words.append(load_tab(1, placed([P, T], U32, "tab_words1", GOT_A + 256 - 4 * T)))
 
-        table_planes = [first_planes[:, :, 0:HALF], second_planes]
-        wc_planes = first_planes[:, :, HALF : HALF + H]
+        table_planes = [
+            [first_planes[:, :, 0:HALF], second_planes],
+            [late_planes[:, :, 0:HALF], late_planes[:, :, HALF + H : ROW]],
+        ]
+        wc_planes = [plane[:, :, HALF : HALF + H] for plane in (first_planes, late_planes)]
         wc_first = placed([P, 2 * H], U16, "wc_first", GOT_A + 256)
         wc_codes = [wc_first[:, H * a : H * (a + 1)] for a in range(2)]
         wc_codes.extend(kept([P, H], U16, f"wc_codes{a}") for a in range(2, PASSES))
@@ -121,8 +130,7 @@ def tile_list_momentum_block_steps_kernel(
             return m, c0, tile
 
         def part_words(m, c0, tile):
-            shape, name = [P, 2, tile.shape[1]], f"v_codes{m}_{c0}"
-            codes = placed(shape, U16, name, GOT_V - 2048) if (m, c0) == (1, 0) else kept(shape, U16, name)
+            codes = kept([P, 2, tile.shape[1]], U16, f"v_codes{m}_{c0}")
             v_codes[m].append((c0, codes))
             nc.vector.tensor_copy(
                 codes[:].rearrange("p h (c i) -> p c h i", i=8),
@@ -133,8 +141,9 @@ def tile_list_momentum_block_steps_kernel(
             m, h = divmod(a, 2)
             b, o = divmod(c0, HALF)
             start, codes = [piece for piece in v_codes[m] if piece[0] <= c0][-1]
-            return codes[:, h, c0 - start : c0 - start + width].bitcast(FP4X4), table_planes[b][:, a, o : o + width]
+            return codes[:, h, c0 - start : c0 - start + width].bitcast(FP4X4), table_planes[m][b][:, h, o : o + width]
 
+        c_acc = [[bank([P, HALF], 4 * b + t) for t in range(4)] for b in range(2)]
 
         def c_passes(m, c0, width):
             b, o = divmod(c0, HALF)
@@ -144,25 +153,13 @@ def tile_list_momentum_block_steps_kernel(
                     nc.tensor.matmul_mx(
                         out=c_acc[b][t][:, o : o + width],
                         lhsT=wc_codes[a][:, P * t : P * (t + 1)].bitcast(FP4X4),
-                        lhsT_scale=wc_planes[:, a, P * t : P * (t + 1)],
+                        lhsT_scale=wc_planes[m][:, a % 2, P * t : P * (t + 1)],
                         rhs=rhs,
                         rhs_scale=rhs_scale,
                         start=(a == 0 and o == 0),
                         stop=(a == PASSES - 1),
                     )
 
-        idle = bank([P, HALF], 7)
-        for w in range(4):
-            nc.tensor.matmul_mx(
-                out=idle[:],
-                lhsT=wc_raw[0][:, 0, 0:P].bitcast(FP4X4),
-                lhsT_scale=wcs_raw[:, 0:P],
-                rhs=wc_raw[0][:, 1, :].bitcast(FP4X4),
-                rhs_scale=wcs_raw[:],
-                start=True,
-                stop=True,
-            )
-        c_acc = [[bank([P, HALF], 4 * b + t) for t in range(4)] for b in range(2)]
         order_wc(0)
         order_wc(1)
         first = gather_words(0, 0, placed([P, QUARTER], U32, "got_q0", GOT_V))
@@ -173,9 +170,11 @@ def tile_list_momentum_block_steps_kernel(
         c_passes(0, QUARTER, QUARTER)
         got_b = placed([P, HALF], U8, "got_b", GOT_V - 256)
         nc.vector.tensor_copy(got_b[:], tab_scale[:].indirect(offsets[:, 32:64]))
-        move_rows(second_planes, got_b, (nc.sync, nc.scalar))
+        move_rows(second_planes, got_b, 0, (nc.sync, nc.sync))
         wc_raw.append(load_wc(1, placed([P, 2, H], U16, "wc_raw1", SCALES - 1024)))
         third = gather_words(0, HALF, placed([P, HALF], U32, "got_b0", GOT_V + 512))
+        nc.vector.tensor_copy(stage[32:64, HALF + H : ROW].bitcast(I32), got_b[32:64, :].bitcast(I32))
+        move_rows(late_planes, stage, 1, (nc.sync, nc.sync))
 
         wd_all = placed([P, PASSES * 4 * H], F32, "wd_all", WD)
         wd_raw = [wd_all[:, 4 * H * a : 4 * H * (a + 1)] for a in range(PASSES)]
@@ -233,15 +232,12 @@ def tile_list_momentum_block_steps_kernel(
                 bias=1.0,
             )
 
-        cast_wd(0, 0, nc.scalar.copy)
-        cast_wd(0, 1, nc.scalar.copy)
         squares(0)
         squares(1)
         rsqrt(0)
         for a in range(PASSES):
-            if a > 0:
-                cast_wd(a, 0, nc.vector.tensor_copy)
-                cast_wd(a, 1, nc.vector.tensor_copy)
+            cast_wd(a, 0, nc.vector.tensor_copy)
+            cast_wd(a, 1, nc.vector.tensor_copy)
             quant_wd(a, 0)
             quant_wd(a, 1)
         for g in range(1, 4):
@@ -342,8 +338,7 @@ def tile_list_momentum_block_steps_kernel(
         for i in range(2):
             d_pass(3, i)
         d_rest(4)
-        for a in d_order(5)[:2]:
-            d_pass(a, 5)
+        d_rest(5)
         for i in range(2, 4):
             d_pass(3, i)
         damp_chunk(0)
@@ -351,8 +346,6 @@ def tile_list_momentum_block_steps_kernel(
         quant_h(0, 2)
         for part in y_cols(0, 2, (7, 0, 1)):
             empty(on_scalar, part, 0)
-        for a in d_order(5)[2:]:
-            d_pass(a, 5)
         d_rest(6)
         for i in (2, 3, 4):
             damp_chunk(i)

@@ -27,10 +27,7 @@ QUARTER = 256
 RUN = 2
 EARLY = 6
 GOT_A = 8192
-GOT_Q = 12288
-SCALES = 15360
-WD = 18432
-GOT_V = WD + 32768 + 128
+GOT_V = GOT_A + 512 + 32768 + 1024
 
 
 def tile_list_momentum_block_steps_kernel(
@@ -55,18 +52,16 @@ def tile_list_momentum_block_steps_kernel(
             return tile.rearrange("p a e -> p (a e)").bitcast(I32).rearrange("p (a e) -> p a e", a=tile.shape[1])
 
         offsets = keep.tile([P, S // 16], U16, name="offsets")
-        tab_scale = placed([P, T], U8, "tab_scale", SCALES)
+        tab_scale = kept([P, T], U8, "tab_scale")
         wcs_raw = kept([P, H], U8, "wcs_raw")
-        first_planes = kept([P, 2, HALF + H], U8, "first_planes")
-        second_planes = kept([P, 2, HALF], U8, "second_planes")
-        late_planes = kept([P, 2, ROW], U8, "late_planes")
+        planes = [kept([P, 2, S + H], U8, f"planes{m}") for m in range(2)]
         warm = keep.tile([P, 2], F32, name="warm")
 
         nc.vector.memset(warm[:, 0:1], 1.0)
         nc.scalar.activation(warm[:, 1:2], warm[:, 0:1], ACT.Abs_reciprocal_sqrt, bias=1.0)
         nc.vector.memset(wcs_raw[64:128, :].bitcast(I32), 0)
         nc.vector.memset(tab_scale[64:128, :].bitcast(I32), 0)
-        for plane in (first_planes, second_planes, late_planes):
+        for plane in planes:
             nc.vector.memset(plane[:].rearrange("p a e -> p (a e)").bitcast(I32), 0)
 
         nc.sync.dma_start(offsets[:], offs)
@@ -95,26 +90,26 @@ def tile_list_momentum_block_steps_kernel(
                 )
 
         tab_words = [load_tab(0, kept([P, T], U32, "tab_words0"))]
-        wc_raw = [load_wc(0, kept([P, 2, H], U16, "wc_raw0"))]
+        wc_raw = [load_wc(m, kept([P, 2, H], U16, f"wc_raw{m}")) for m in range(2)]
 
-        stage = kept([P, ROW], U8, "stage")
-        got_a = placed([P, HALF], U8, "got_a", GOT_A)
-        nc.vector.tensor_copy(got_a[:], tab_scale[:].indirect(offsets[:, 0:32]))
+        stage = kept([P, S + H], U8, "stage")
+        got = placed([P, S], U8, "got", GOT_A)
+        nc.vector.tensor_copy(got[:], tab_scale[:].indirect(offsets[:]))
         nc.vector.tensor_copy(
-            stage[:, HALF : HALF + H].rearrange("p (t c i) -> p c t i", t=4, i=16),
+            stage[:, S : S + H].rearrange("p (t c i) -> p c t i", t=4, i=16),
             wcs_raw[:].rearrange("p (c i t) -> p c t i", t=4, i=16),
         )
-        nc.vector.tensor_copy(stage[0:64, 0:HALF].bitcast(I32), got_a[0:64, :].bitcast(I32))
-        move_rows(first_planes, stage[:, 0 : HALF + H], 0, (nc.sync, nc.sync))
+        nc.vector.tensor_copy(stage[0:64, 0:S].bitcast(I32), got[0:64, :].bitcast(I32))
+        move_rows(planes[0], stage, 0, (nc.sync, nc.sync))
         tab_words.append(load_tab(1, placed([P, T], U32, "tab_words1", GOT_A + 256 - 4 * T)))
+        move_rows(planes[1], stage, 1, (nc.sync, nc.sync))
+        wd_all = placed([P, PASSES * 4 * H], F32, "wd_all", GOT_A + 512)
+        wd_raw = [wd_all[:, 4 * H * a : 4 * H * (a + 1)] for a in range(PASSES)]
+        for a in range(PASSES):
+            nc.sync.dma_start(wd_raw[a], wd[512 * a : 512 * (a + 1), :].rearrange("(p i) r -> p (i r)", i=4))
 
-        table_planes = [
-            [first_planes[:, :, 0:HALF], second_planes],
-            [late_planes[:, :, 0:HALF], late_planes[:, :, HALF + H : ROW]],
-        ]
-        wc_planes = [plane[:, :, HALF : HALF + H] for plane in (first_planes, late_planes)]
-        wc_first = placed([P, 2 * H], U16, "wc_first", GOT_A + 256)
-        wc_codes = [wc_first[:, H * a : H * (a + 1)] for a in range(2)]
+        wc_planes = [plane[:, :, S : S + H] for plane in planes]
+        wc_codes = [kept([P, H], U16, f"wc_codes{a}") for a in range(2)]
         wc_codes.extend(kept([P, H], U16, f"wc_codes{a}") for a in range(2, PASSES))
         v_codes = [[], []]
 
@@ -139,11 +134,9 @@ def tile_list_momentum_block_steps_kernel(
 
         def v_operand(a, c0, width):
             m, h = divmod(a, 2)
-            b, o = divmod(c0, HALF)
             start, codes = [piece for piece in v_codes[m] if piece[0] <= c0][-1]
-            return codes[:, h, c0 - start : c0 - start + width].bitcast(FP4X4), table_planes[m][b][:, h, o : o + width]
+            return codes[:, h, c0 - start : c0 - start + width].bitcast(FP4X4), planes[m][:, h, c0 : c0 + width]
 
-        c_acc = [[bank([P, HALF], 4 * b + t) for t in range(4)] for b in range(2)]
 
         def c_passes(m, c0, width):
             b, o = divmod(c0, HALF)
@@ -157,42 +150,39 @@ def tile_list_momentum_block_steps_kernel(
                         rhs=rhs,
                         rhs_scale=rhs_scale,
                         start=(a == 0 and o == 0),
-                        stop=(a == PASSES - 1),
+                        stop=(a == PASSES - 1 and o + width == HALF),
                     )
 
+        idle = bank([P, HALF], 7)
+        for w in range(4):
+            nc.tensor.matmul_mx(
+                out=idle[:],
+                lhsT=wc_raw[0][:, 0, 0:P].bitcast(FP4X4),
+                lhsT_scale=wcs_raw[:, 0:P],
+                rhs=wc_raw[0][:, 1, :].bitcast(FP4X4),
+                rhs_scale=wcs_raw[:],
+                start=True,
+                stop=True,
+            )
+        c_acc = [[bank([P, HALF], 4 * b + t) for t in range(4)] for b in range(2)]
         order_wc(0)
         order_wc(1)
-        first = gather_words(0, 0, placed([P, QUARTER], U32, "got_q0", GOT_V))
-        second = gather_words(0, QUARTER, placed([P, QUARTER], U32, "got_q1", GOT_Q))
-        part_words(*first)
-        c_passes(0, 0, QUARTER)
-        part_words(*second)
-        c_passes(0, QUARTER, QUARTER)
-        got_b = placed([P, HALF], U8, "got_b", GOT_V - 256)
-        nc.vector.tensor_copy(got_b[:], tab_scale[:].indirect(offsets[:, 32:64]))
-        move_rows(second_planes, got_b, 0, (nc.sync, nc.sync))
-        wc_raw.append(load_wc(1, placed([P, 2, H], U16, "wc_raw1", SCALES - 1024)))
-        third = gather_words(0, HALF, placed([P, HALF], U32, "got_b0", GOT_V + 512))
-        nc.vector.tensor_copy(stage[32:64, HALF + H : ROW].bitcast(I32), got_b[32:64, :].bitcast(I32))
-        move_rows(late_planes, stage, 1, (nc.sync, nc.sync))
-
-        wd_all = placed([P, PASSES * 4 * H], F32, "wd_all", WD)
-        wd_raw = [wd_all[:, 4 * H * a : 4 * H * (a + 1)] for a in range(PASSES)]
-        for a in range(PASSES):
-            nc.sync.dma_start(wd_raw[a], wd[512 * a : 512 * (a + 1), :].rearrange("(p i) r -> p (i r)", i=4))
-
-        part_words(*third)
-        c_passes(0, HALF, HALF)
         order_wc(2)
         order_wc(3)
-        for b in range(2):
-            part_words(*gather_words(1, HALF * b, placed([P, HALF], U32, f"got_1{b}", GOT_V + 2048)))
-            c_passes(1, HALF * b, HALF)
+        for m in range(2):
+            first = gather_words(m, 0, placed([P, QUARTER], U32, f"got{m}_first", GOT_V))
+            second = gather_words(m, QUARTER, placed([P, QUARTER], U32, f"got{m}_second", GOT_V + (2048, 1024)[m]))
+            part_words(*first)
+            c_passes(m, 0, QUARTER)
+            third = gather_words(m, HALF, placed([P, HALF], U32, f"got{m}_third", GOT_V - 1024 * m))
+            part_words(*second)
+            c_passes(m, QUARTER, QUARTER)
+            part_words(*third)
+            c_passes(m, HALF, HALF)
 
         wo_codes = placed([P, N], U32, "wo_codes", 0)
         nc.sync.dma_start(wo_codes[:].bitcast(I32), wo_words[0].rearrange("p e i -> p (e i)").bitcast(I32))
         wos = placed([P, N], U8, "wos", 4096)
-        nc.vector.memset(wos[:].bitcast(I32), 0)
         for r in range(4):
             nc.sync.dma_start(wos[r:P:32, :].bitcast(I32), wo_scales[0, r:16:4, :].bitcast(I32))
         rate_sb = placed([P, NT], F32, "rate_sb", 5120)

@@ -1,6 +1,7 @@
 from contextlib import ExitStack
 
 import concourse.mybir as mybir
+from concourse.masks import make_identity
 
 K, H, N, T, S = 2048, 512, 768, 2048, 1024
 FLOPS = 2 * K * H * S * 2 + 2 * H * N * S
@@ -25,7 +26,7 @@ NT = N // P
 ROW = HALF + H + HALF
 QUARTER = 256
 RUN = 2
-EARLY = 6
+EARLY = 5
 GOT_A = 8192
 GOT_V = GOT_A + 512 + 32768 + 1024
 
@@ -75,6 +76,16 @@ def tile_list_momentum_block_steps_kernel(
                 wcs_raw[32 * m : 32 * (m + 1), :].bitcast(I32), wc_scales.bitcast(I32)[2 * m : 2 * m + 2].rearrange("h q e -> q h e")
             )
 
+        rate_rows = kept([P, P], F32, "rate_rows")
+        nc.vector.memset(rate_rows[:], 0.0)
+        nc.scalar.dma_start(rate_rows[0:NT, :], rate.rearrange("(u p) -> u p", p=P))
+        identity = kept([P, P], F32, "identity")
+        make_identity(nc, identity[:])
+        turned = bank([P, P], 6)
+        nc.tensor.transpose(turned[:], rate_rows[:], identity[:])
+        rate_sb = kept([P, NT], F32, "rate_sb")
+        nc.scalar.copy(rate_sb[:], turned[:, 0:NT])
+
         def load_wc(m, raw):
             nc.sync.dma_start(words(raw[:]), wc_words.bitcast(I32)[2 * m : 2 * m + 2].rearrange("a p e -> p a e"))
             return raw
@@ -100,7 +111,7 @@ def tile_list_momentum_block_steps_kernel(
             wcs_raw[:].rearrange("p (c i t) -> p c t i", t=4, i=16),
         )
         nc.vector.tensor_copy(stage[0:64, 0:S].bitcast(I32), got[0:64, :].bitcast(I32))
-        move_rows(planes[0], stage, 0, (nc.sync, nc.sync))
+        move_rows(planes[0], stage, 0, (nc.sync, nc.scalar))
         tab_words.append(load_tab(1, placed([P, T], U32, "tab_words1", GOT_A + 256 - 4 * T)))
         move_rows(planes[1], stage, 1, (nc.sync, nc.sync))
         wd_all = placed([P, PASSES * 4 * H], F32, "wd_all", GOT_A + 512)
@@ -185,9 +196,6 @@ def tile_list_momentum_block_steps_kernel(
         wos = placed([P, N], U8, "wos", 4096)
         for r in range(4):
             nc.sync.dma_start(wos[r:P:32, :].bitcast(I32), wo_scales[0, r:16:4, :].bitcast(I32))
-        rate_sb = placed([P, NT], F32, "rate_sb", 5120)
-        with nc.allow_non_contiguous_dma(reason="one rate for each output row"):
-            nc.sync.dma_start(rate_sb[:], rate.rearrange("(u p) -> p u", p=P))
 
         wd_bf = [[kept([P, 2, P, 4], BF16, f"wd_bf{a}{s}") for s in range(2)] for a in range(PASSES)]
         wd_codes = [kept([P, H], U32, f"wd_codes{a}") for a in range(PASSES)]
@@ -328,13 +336,19 @@ def tile_list_momentum_block_steps_kernel(
         for i in range(2):
             d_pass(3, i)
         d_rest(4)
-        d_rest(5)
+        for a in d_order(5)[:2]:
+            d_pass(a, 5)
         for i in range(2, 4):
             d_pass(3, i)
+        for a in d_order(5)[2:]:
+            d_pass(a, 5)
         damp_chunk(0)
         damp_chunk(1)
         quant_h(0, 2)
-        for part in y_cols(0, 2, (7, 0, 1)):
+        pair0 = y_cols(0, 2, (7, 0, 1))
+        for e in range(2):
+            empty(on_scalar, (pair0[0][0][:, e : e + 1, :], e), 0)
+        for part in pair0[1:]:
             empty(on_scalar, part, 0)
         d_rest(6)
         for i in (2, 3, 4):
@@ -346,7 +360,7 @@ def tile_list_momentum_block_steps_kernel(
         quant_h(4, 2)
         quant_h(6, 1)
         empty(on_scalar, pair1[0], PAIR)
-        empty(on_vector, pair1[1], PAIR)
+        empty(on_scalar, pair1[1], PAIR)
         empty(on_vector, pair1[2], PAIR)
         d_rest(7)
         pair2 = y_cols(4, 2, (0, 1, 5))

@@ -1,7 +1,6 @@
 from contextlib import ExitStack
 
 import concourse.mybir as mybir
-from concourse.masks import make_identity
 
 K, H, N, T, S = 2048, 512, 768, 2048, 1024
 FLOPS = 2 * K * H * S * 2 + 2 * H * N * S
@@ -23,12 +22,12 @@ HALF = 512
 CHUNK = 128
 PAIR = 256
 NT = N // P
-ROW = HALF + H + HALF
 QUARTER = 256
 RUN = 2
 EARLY = 5
-GOT_A = 8192
-GOT_V = GOT_A + 512 + 32768 + 1024
+WARM_UPS = 3
+GOT_V = 8192
+WD_AT = 18432
 
 
 def tile_list_momentum_block_steps_kernel(
@@ -54,13 +53,13 @@ def tile_list_momentum_block_steps_kernel(
 
         offsets = keep.tile([P, S // 16], U16, name="offsets")
         tab_scale = kept([P, T], U8, "tab_scale")
-        wcs_raw = kept([P, H], U8, "wcs_raw")
-        planes = [kept([P, 2, S + H], U8, f"planes{m}") for m in range(2)]
+        wcs_raw = kept([P, PASSES, H], U8, "wcs_raw")
+        planes = [kept([P, 2, S], U8, f"planes{m}") for m in range(2)]
         warm = keep.tile([P, 2], F32, name="warm")
 
         nc.vector.memset(warm[:, 0:1], 1.0)
         nc.scalar.activation(warm[:, 1:2], warm[:, 0:1], ACT.Abs_reciprocal_sqrt, bias=1.0)
-        nc.vector.memset(wcs_raw[64:128, :].bitcast(I32), 0)
+        nc.vector.memset(wcs_raw[:].rearrange("p a e -> p (a e)").bitcast(I32), 0)
         nc.vector.memset(tab_scale[64:128, :].bitcast(I32), 0)
         for plane in planes:
             nc.vector.memset(plane[:].rearrange("p a e -> p (a e)").bitcast(I32), 0)
@@ -71,58 +70,40 @@ def tile_list_momentum_block_steps_kernel(
                 tab_scale[32 * m : 32 * (m + 1), :].bitcast(I32),
                 tab[m, 512 * T :].rearrange("(h q t) -> q h t", h=2, q=16).bitcast(I32),
             )
-        for m in range(2):
-            nc.sync.dma_start(
-                wcs_raw[32 * m : 32 * (m + 1), :].bitcast(I32), wc_scales.bitcast(I32)[2 * m : 2 * m + 2].rearrange("h q e -> q h e")
+        for q in (0, 2, 1, 3):
+            nc.scalar.dma_start(
+                words(wcs_raw[32 * q : 32 * q + 4]), wc_scales.bitcast(I32)[:, 4 * q : 4 * q + 4, :].rearrange("a r e -> r a e")
             )
-
-        rate_rows = kept([P, P], F32, "rate_rows")
-        nc.vector.memset(rate_rows[:], 0.0)
-        nc.scalar.dma_start(rate_rows[0:NT, :], rate.rearrange("(u p) -> u p", p=P))
-        identity = kept([P, P], F32, "identity")
-        make_identity(nc, identity[:])
-        turned = bank([P, P], 6)
-        nc.tensor.transpose(turned[:], rate_rows[:], identity[:])
-        rate_sb = kept([P, NT], F32, "rate_sb")
-        nc.scalar.copy(rate_sb[:], turned[:, 0:NT])
-
-        def load_wc(m, raw):
-            nc.sync.dma_start(words(raw[:]), wc_words.bitcast(I32)[2 * m : 2 * m + 2].rearrange("a p e -> p a e"))
-            return raw
 
         def load_tab(m, tile):
             nc.sync.dma_start(tile[:].bitcast(I32), tab[m, 0 : 512 * T].rearrange("(p w) -> p w", p=P).bitcast(I32))
             return tile
 
-        def move_rows(plane, rows, m, queues):
-            for q in (0, 2, 1, 3):
-                queues[q // 2].dma_start(
-                    words(plane[32 * q : 32 * q + 4]), rows[32 * m + 8 * q : 32 * m + 8 * (q + 1), :].bitcast(I32)
-                )
+        def load_wc(m, raw):
+            nc.sync.dma_start(words(raw[:]), wc_words.bitcast(I32)[2 * m : 2 * m + 2].rearrange("a p e -> p a e"))
+            return raw
 
         tab_words = [load_tab(0, kept([P, T], U32, "tab_words0"))]
         wc_raw = [load_wc(m, kept([P, 2, H], U16, f"wc_raw{m}")) for m in range(2)]
 
-        stage = kept([P, S + H], U8, "stage")
-        got = placed([P, S], U8, "got", GOT_A)
+        got = kept([P, S], U8, "got")
         nc.vector.tensor_copy(got[:], tab_scale[:].indirect(offsets[:]))
-        nc.vector.tensor_copy(
-            stage[:, S : S + H].rearrange("p (t c i) -> p c t i", t=4, i=16),
-            wcs_raw[:].rearrange("p (c i t) -> p c t i", t=4, i=16),
-        )
-        nc.vector.tensor_copy(stage[0:64, 0:S].bitcast(I32), got[0:64, :].bitcast(I32))
-        move_rows(planes[0], stage, 0, (nc.sync, nc.scalar))
-        tab_words.append(load_tab(1, placed([P, T], U32, "tab_words1", GOT_A + 256 - 4 * T)))
-        move_rows(planes[1], stage, 1, (nc.sync, nc.sync))
-        wd_all = placed([P, PASSES * 4 * H], F32, "wd_all", GOT_A + 512)
-        wd_raw = [wd_all[:, 4 * H * a : 4 * H * (a + 1)] for a in range(PASSES)]
-        for a in range(PASSES):
-            nc.sync.dma_start(wd_raw[a], wd[512 * a : 512 * (a + 1), :].rearrange("(p i) r -> p (i r)", i=4))
 
-        wc_planes = [plane[:, :, S : S + H] for plane in planes]
-        wc_codes = [kept([P, H], U16, f"wc_codes{a}") for a in range(2)]
-        wc_codes.extend(kept([P, H], U16, f"wc_codes{a}") for a in range(2, PASSES))
-        v_codes = [[], []]
+        def move_rows(m, queues):
+            for q in (0, 2, 1, 3):
+                queues[q // 2].dma_start(
+                    words(planes[m][32 * q : 32 * q + 4]), got[32 * m + 8 * q : 32 * m + 8 * (q + 1), :].bitcast(I32)
+                )
+
+        move_rows(0, (nc.sync, nc.scalar))
+        tab_words.append(load_tab(1, placed([P, T], U32, "tab_words1", 0)))
+        move_rows(1, (nc.sync, nc.sync))
+        wd_raw = [placed([P, 4 * H], F32, f"wd_raw{a}", WD_AT + 4096 + 8192 * a + 4096 * min(a, 1)) for a in range(PASSES)]
+        for a in range(PASSES):
+            nc.sync.dma_start(wd_raw[a][:], wd[512 * a : 512 * (a + 1), :].rearrange("(p i) r -> p (i r)", i=4))
+
+        wc_codes = [kept([P, H], U16, f"wc_codes{a}") for a in range(PASSES)]
+        wc_planes = {}
 
         def order_wc(a):
             nc.scalar.copy(
@@ -130,72 +111,95 @@ def tile_list_momentum_block_steps_kernel(
                 wc_raw[a // 2][:, a % 2, :].rearrange("p (c i t) -> p c t i", t=4, i=8),
             )
 
+        def order_wc_scale(a, offset):
+            wc_planes[a] = placed([P, H], U8, f"wc_plane{a}", offset)
+            nc.vector.tensor_copy(
+                wc_planes[a][:].rearrange("p (t c i) -> p c t i", t=4, i=16),
+                wcs_raw[:, a, :].rearrange("p (c i t) -> p c t i", t=4, i=16),
+            )
+
+        for a in range(PASSES):
+            order_wc(a)
+
+        v_planes = [planes[a // 2][:, a % 2, :] for a in range(PASSES)]
+        v_codes = [[kept([P, 2, HALF], U16, f"v_codes{m}{b}") for b in range(2)] for m in range(2)]
+
         def gather_words(m, c0, tile):
             width = tile.shape[1]
             nc.vector.tensor_copy(tile[:], tab_words[m][:].indirect(offsets[:, c0 // 16 : (c0 + width) // 16]))
             return m, c0, tile
 
         def part_words(m, c0, tile):
-            codes = kept([P, 2, tile.shape[1]], U16, f"v_codes{m}_{c0}")
-            v_codes[m].append((c0, codes))
+            b, o = divmod(c0, HALF)
             nc.vector.tensor_copy(
-                codes[:].rearrange("p h (c i) -> p c h i", i=8),
+                v_codes[m][b][:, :, o : o + tile.shape[1]].rearrange("p h (c i) -> p c h i", i=8),
                 tile[:].bitcast(U16).rearrange("p (c i h) -> p c h i", i=8, h=2),
             )
 
         def v_operand(a, c0, width):
             m, h = divmod(a, 2)
-            start, codes = [piece for piece in v_codes[m] if piece[0] <= c0][-1]
-            return codes[:, h, c0 - start : c0 - start + width].bitcast(FP4X4), planes[m][:, h, c0 : c0 + width]
-
-
-        def c_passes(m, c0, width):
             b, o = divmod(c0, HALF)
-            for a in (2 * m, 2 * m + 1):
-                for t in range(4):
-                    rhs, rhs_scale = v_operand(a, c0, width)
-                    nc.tensor.matmul_mx(
-                        out=c_acc[b][t][:, o : o + width],
-                        lhsT=wc_codes[a][:, P * t : P * (t + 1)].bitcast(FP4X4),
-                        lhsT_scale=wc_planes[m][:, a % 2, P * t : P * (t + 1)],
-                        rhs=rhs,
-                        rhs_scale=rhs_scale,
-                        start=(a == 0 and o == 0),
-                        stop=(a == PASSES - 1 and o + width == HALF),
-                    )
+            return v_codes[m][b][:, h, o : o + width].bitcast(FP4X4), v_planes[a][:, c0 : c0 + width]
 
         idle = bank([P, HALF], 7)
-        for w in range(4):
+        wc_bytes = wcs_raw[:].rearrange("p a e -> p (a e)")
+        for w in range(WARM_UPS):
             nc.tensor.matmul_mx(
                 out=idle[:],
-                lhsT=wc_raw[0][:, 0, 0:P].bitcast(FP4X4),
-                lhsT_scale=wcs_raw[:, 0:P],
-                rhs=wc_raw[0][:, 1, :].bitcast(FP4X4),
-                rhs_scale=wcs_raw[:],
+                lhsT=wc_bytes[:, 0 : 2 * P].bitcast(FP4X4),
+                lhsT_scale=wc_bytes[:, 0:P],
+                rhs=wc_bytes[:, 0 : 2 * HALF].bitcast(FP4X4),
+                rhs_scale=wc_bytes[:, 0:HALF],
                 start=True,
                 stop=True,
             )
         c_acc = [[bank([P, HALF], 4 * b + t) for t in range(4)] for b in range(2)]
-        order_wc(0)
-        order_wc(1)
-        order_wc(2)
-        order_wc(3)
-        for m in range(2):
-            first = gather_words(m, 0, placed([P, QUARTER], U32, f"got{m}_first", GOT_V))
-            second = gather_words(m, QUARTER, placed([P, QUARTER], U32, f"got{m}_second", GOT_V + (2048, 1024)[m]))
-            part_words(*first)
-            c_passes(m, 0, QUARTER)
-            third = gather_words(m, HALF, placed([P, HALF], U32, f"got{m}_third", GOT_V - 1024 * m))
-            part_words(*second)
-            c_passes(m, QUARTER, QUARTER)
-            part_words(*third)
-            c_passes(m, HALF, HALF)
 
+        def c_pass(a, c0, width):
+            b, o = divmod(c0, HALF)
+            rhs, rhs_scale = v_operand(a, c0, width)
+            for t in range(4):
+                nc.tensor.matmul_mx(
+                    out=c_acc[b][t][:, o : o + width],
+                    lhsT=wc_codes[a][:, P * t : P * (t + 1)].bitcast(FP4X4),
+                    lhsT_scale=wc_planes[a][:, P * t : P * (t + 1)],
+                    rhs=rhs,
+                    rhs_scale=rhs_scale,
+                    start=(a == 0 and o == 0),
+                    stop=(a == PASSES - 1),
+                )
+
+        def in_quarters(m, b, at):
+            pieces = [
+                gather_words(m, HALF * b + QUARTER * e, placed([P, QUARTER], U32, f"got{m}{b}{e}", at[e])) for e in range(2)
+            ]
+            for piece in pieces:
+                part_words(*piece)
+
+        in_quarters(0, 0, (GOT_V + 2048, GOT_V + 5632))
+        order_wc_scale(0, GOT_V + 2048)
+        order_wc_scale(1, GOT_V + 2560)
+        c_pass(0, 0, HALF)
+        c_pass(1, 0, HALF)
+        piece = gather_words(0, HALF, placed([P, HALF], U32, "got01", GOT_V + 3840))
+        order_wc_scale(2, GOT_V + 5888)
+        part_words(*piece)
+        order_wc_scale(3, GOT_V + 6400)
+        c_pass(0, HALF, HALF)
+        c_pass(1, HALF, HALF)
+        for b in range(2):
+            in_quarters(1, b, (GOT_V, GOT_V + 1024))
+            c_pass(2, HALF * b, HALF)
+            c_pass(3, HALF * b, HALF)
+
+        rate_sb = kept([P, NT], F32, "rate_sb")
         wo_codes = placed([P, N], U32, "wo_codes", 0)
         nc.sync.dma_start(wo_codes[:].bitcast(I32), wo_words[0].rearrange("p e i -> p (e i)").bitcast(I32))
         wos = placed([P, N], U8, "wos", 4096)
         for r in range(4):
             nc.sync.dma_start(wos[r:P:32, :].bitcast(I32), wo_scales[0, r:16:4, :].bitcast(I32))
+        with nc.allow_non_contiguous_dma(reason="one rate for each partition and row tile"):
+            nc.sync.dma_start(rate_sb[:], rate.rearrange("(u p) -> p u", p=P))
 
         wd_bf = [[kept([P, 2, P, 4], BF16, f"wd_bf{a}{s}") for s in range(2)] for a in range(PASSES)]
         wd_codes = [kept([P, H], U32, f"wd_codes{a}") for a in range(PASSES)]
@@ -204,7 +208,7 @@ def tile_list_momentum_block_steps_kernel(
         def cast_wd(a, s, copy):
             copy(
                 wd_bf[a][s][:].rearrange("p t m i -> p m i t"),
-                wd_raw[a].rearrange("p (i m t) -> p m i t", i=4, t=4)[:, :, :, 2 * s : 2 * s + 2],
+                wd_raw[a][:].rearrange("p (i m t) -> p m i t", i=4, t=4)[:, :, :, 2 * s : 2 * s + 2],
             )
 
         def quant_wd(a, s):
@@ -214,7 +218,7 @@ def tile_list_momentum_block_steps_kernel(
                 in_=wd_bf[a][s][:].rearrange("p t m i -> p (t m i)"),
             )
 
-        sq = [kept([P, 4, HALF], F32, f"sq{b}") for b in range(2)]
+        sq = [placed([P, 4, HALF], F32, f"sq{b}", WD_AT + 8192 * b) for b in range(2)]
         damp = [kept([P, PAIR // RUN, 4, RUN], F32, f"damp{g}") for g in range(S // PAIR)]
 
         def squares(b):
@@ -230,12 +234,15 @@ def tile_list_momentum_block_steps_kernel(
                 bias=1.0,
             )
 
+        cast_wd(0, 0, nc.scalar.copy)
+        cast_wd(0, 1, nc.scalar.copy)
         squares(0)
         squares(1)
         rsqrt(0)
         for a in range(PASSES):
-            cast_wd(a, 0, nc.vector.tensor_copy)
-            cast_wd(a, 1, nc.vector.tensor_copy)
+            if a > 0:
+                cast_wd(a, 0, nc.vector.tensor_copy)
+                cast_wd(a, 1, nc.vector.tensor_copy)
             quant_wd(a, 0)
             quant_wd(a, 1)
         for g in range(1, 4):

@@ -28,6 +28,7 @@ EARLY = 5
 WARM_UPS = 3
 GOT_V = 8192
 WD_AT = 18432
+ROWS_AT = WD_AT + 40960
 
 
 def tile_list_momentum_block_steps_kernel(
@@ -52,28 +53,24 @@ def tile_list_momentum_block_steps_kernel(
             return tile.rearrange("p a e -> p (a e)").bitcast(I32).rearrange("p (a e) -> p a e", a=tile.shape[1])
 
         offsets = keep.tile([P, S // 16], U16, name="offsets")
-        tab_scale = kept([P, T], U8, "tab_scale")
+        tab_scale = placed([P, T], U8, "tab_scale", ROWS_AT)
         wcs_raw = kept([P, PASSES, H], U8, "wcs_raw")
-        planes = [kept([P, 2, S], U8, f"planes{m}") for m in range(2)]
         warm = keep.tile([P, 2], F32, name="warm")
 
         nc.vector.memset(warm[:, 0:1], 1.0)
         nc.scalar.activation(warm[:, 1:2], warm[:, 0:1], ACT.Abs_reciprocal_sqrt, bias=1.0)
         nc.vector.memset(wcs_raw[:].rearrange("p a e -> p (a e)").bitcast(I32), 0)
-        nc.vector.memset(tab_scale[64:128, :].bitcast(I32), 0)
-        for plane in planes:
-            nc.vector.memset(plane[:].rearrange("p a e -> p (a e)").bitcast(I32), 0)
+        for m in range(2):
+            nc.vector.memset(tab_scale[64 * m + 32 : 64 * m + 64, :].bitcast(I32), 0)
 
         nc.sync.dma_start(offsets[:], offs)
         for m in range(2):
             nc.sync.dma_start(
-                tab_scale[32 * m : 32 * (m + 1), :].bitcast(I32),
+                tab_scale[64 * m : 64 * m + 32, :].bitcast(I32),
                 tab[m, 512 * T :].rearrange("(h q t) -> q h t", h=2, q=16).bitcast(I32),
             )
-        for q in (0, 2, 1, 3):
-            nc.scalar.dma_start(
-                words(wcs_raw[32 * q : 32 * q + 4]), wc_scales.bitcast(I32)[:, 4 * q : 4 * q + 4, :].rearrange("a r e -> r a e")
-            )
+        for r in range(4):
+            nc.scalar.dma_start(words(wcs_raw[r:P:32]), wc_scales.bitcast(I32)[:, r:16:4, :].rearrange("a q e -> q a e"))
 
         def load_tab(m, tile):
             nc.sync.dma_start(tile[:].bitcast(I32), tab[m, 0 : 512 * T].rearrange("(p w) -> p w", p=P).bitcast(I32))
@@ -84,26 +81,23 @@ def tile_list_momentum_block_steps_kernel(
             return raw
 
         tab_words = [load_tab(0, kept([P, T], U32, "tab_words0"))]
-        wc_raw = [load_wc(m, kept([P, 2, H], U16, f"wc_raw{m}")) for m in range(2)]
+        wc_raw = [load_wc(m, placed([P, 2, H], U16, f"wc_raw{m}", ROWS_AT + 2048 * (m + 1))) for m in range(2)]
 
         got = kept([P, S], U8, "got")
         nc.vector.tensor_copy(got[:], tab_scale[:].indirect(offsets[:]))
 
+        planes = []
+
         def move_rows(m, queues):
+            planes.append(placed([P, 2, S], U8, f"planes{m}", ROWS_AT + 2048 * m))
             for q in (0, 2, 1, 3):
                 queues[q // 2].dma_start(
-                    words(planes[m][32 * q : 32 * q + 4]), got[32 * m + 8 * q : 32 * m + 8 * (q + 1), :].bitcast(I32)
+                    words(planes[m][32 * q : 32 * q + 4]), got[64 * m + 8 * q : 64 * m + 8 * (q + 1), :].bitcast(I32)
                 )
 
         move_rows(0, (nc.sync, nc.scalar))
         tab_words.append(load_tab(1, placed([P, T], U32, "tab_words1", 0)))
-        move_rows(1, (nc.sync, nc.sync))
-        wd_raw = [placed([P, 4 * H], F32, f"wd_raw{a}", WD_AT + 4096 + 8192 * a + 4096 * min(a, 1)) for a in range(PASSES)]
-        for a in range(PASSES):
-            nc.sync.dma_start(wd_raw[a][:], wd[512 * a : 512 * (a + 1), :].rearrange("(p i) r -> p (i r)", i=4))
-
         wc_codes = [kept([P, H], U16, f"wc_codes{a}") for a in range(PASSES)]
-        wc_planes = {}
 
         def order_wc(a):
             nc.scalar.copy(
@@ -111,15 +105,21 @@ def tile_list_momentum_block_steps_kernel(
                 wc_raw[a // 2][:, a % 2, :].rearrange("p (c i t) -> p c t i", t=4, i=8),
             )
 
+        for a in range(PASSES):
+            order_wc(a)
+        move_rows(1, (nc.sync, nc.scalar))
+        wd_raw = [placed([P, 4 * H], F32, f"wd_raw{a}", WD_AT + 4096 + 8192 * a + 4096 * min(a, 1)) for a in range(PASSES)]
+        for a in range(PASSES):
+            nc.sync.dma_start(wd_raw[a][:], wd[512 * a : 512 * (a + 1), :].rearrange("(p i) r -> p (i r)", i=4))
+
+        wc_planes = {}
+
         def order_wc_scale(a, offset):
             wc_planes[a] = placed([P, H], U8, f"wc_plane{a}", offset)
             nc.vector.tensor_copy(
                 wc_planes[a][:].rearrange("p (t c i) -> p c t i", t=4, i=16),
                 wcs_raw[:, a, :].rearrange("p (c i t) -> p c t i", t=4, i=16),
             )
-
-        for a in range(PASSES):
-            order_wc(a)
 
         v_planes = [planes[a // 2][:, a % 2, :] for a in range(PASSES)]
         v_codes = [[kept([P, 2, HALF], U16, f"v_codes{m}{b}") for b in range(2)] for m in range(2)]

@@ -28,7 +28,7 @@ EARLY = 5
 WARM_UPS = 3
 GOT_V = 8192
 WD_AT = 18432
-ROWS_AT = WD_AT + 40960
+ROWS_AT = WD_AT + 16384
 
 
 def tile_list_momentum_block_steps_kernel(
@@ -108,9 +108,14 @@ def tile_list_momentum_block_steps_kernel(
         for a in range(PASSES):
             order_wc(a)
         move_rows(1, (nc.sync, nc.scalar))
-        wd_raw = [placed([P, 4 * H], F32, f"wd_raw{a}", WD_AT + 4096 + 8192 * a + 4096 * min(a, 1)) for a in range(PASSES)]
-        for a in range(PASSES):
-            nc.sync.dma_start(wd_raw[a][:], wd[512 * a : 512 * (a + 1), :].rearrange("(p i) r -> p (i r)", i=4))
+        wd_rows = [wd[512 * a : 512 * (a + 1), :].rearrange("(p i) r -> p i r", i=4) for a in range(PASSES)]
+        wd_raw = {(a, 0): kept([P, 4, H], F32, f"wd_raw{a}") for a in range(1, PASSES)}
+        wd_raw[0, 0] = kept([P, 4, H // 2], F32, "wd_raw0_left")
+        wd_raw[0, H // 2] = placed([P, 4, H // 2], F32, "wd_raw0_right", WD_AT + 6144)
+        for r0 in (0, H // 2):
+            nc.sync.dma_start(wd_raw[0, r0][:], wd_rows[0][:, :, r0 : r0 + H // 2])
+        for a in range(1, PASSES):
+            nc.sync.dma_start(wd_raw[a, 0][:], wd_rows[a])
 
         wc_planes = {}
 
@@ -205,11 +210,13 @@ def tile_list_momentum_block_steps_kernel(
         wd_codes = [kept([P, H], U32, f"wd_codes{a}") for a in range(PASSES)]
         wd_scale = [kept([P, H], U8, f"wd_scale{a}") for a in range(PASSES)]
 
-        def cast_wd(a, s, copy):
-            copy(
-                wd_bf[a][s][:].rearrange("p t m i -> p m i t"),
-                wd_raw[a][:].rearrange("p (i m t) -> p m i t", i=4, t=4)[:, :, :, 2 * s : 2 * s + 2],
-            )
+        def cast_wd(a, r0, copy):
+            raw = wd_raw[a, r0]
+            for s in range(2):
+                copy(
+                    wd_bf[a][s][:, :, r0 // 4 : (r0 + raw.shape[2]) // 4, :].rearrange("p t m i -> p m i t"),
+                    raw[:].rearrange("p i (m t) -> p m i t", t=4)[:, :, :, 2 * s : 2 * s + 2],
+                )
 
         def quant_wd(a, s):
             nc.vector.quantize_mx(
@@ -235,14 +242,13 @@ def tile_list_momentum_block_steps_kernel(
             )
 
         cast_wd(0, 0, nc.scalar.copy)
-        cast_wd(0, 1, nc.scalar.copy)
+        cast_wd(0, H // 2, nc.scalar.copy)
         squares(0)
         squares(1)
         rsqrt(0)
         for a in range(PASSES):
             if a > 0:
                 cast_wd(a, 0, nc.vector.tensor_copy)
-                cast_wd(a, 1, nc.vector.tensor_copy)
             quant_wd(a, 0)
             quant_wd(a, 1)
         for g in range(1, 4):

@@ -107,7 +107,7 @@ def tile_list_momentum_block_steps_kernel(
 
         for a in range(PASSES):
             order_wc(a)
-        move_rows(1, (nc.sync, nc.scalar))
+        move_rows(1, (nc.sync, nc.sync))
         wd_rows = [wd[512 * a : 512 * (a + 1), :].rearrange("(p i) r -> p i r", i=4) for a in range(PASSES)]
         wd_raw = {(a, 0): kept([P, 4, H], F32, f"wd_raw{a}") for a in range(1, PASSES)}
         wd_raw[0, 0] = kept([P, 4, H // 2], F32, "wd_raw0_left")
@@ -189,13 +189,15 @@ def tile_list_momentum_block_steps_kernel(
         piece = gather_words(0, HALF, placed([P, HALF], U32, "got01", GOT_V + 3840))
         order_wc_scale(2, GOT_V + 5888)
         part_words(*piece)
-        order_wc_scale(3, GOT_V + 6400)
         c_pass(0, HALF, HALF)
         c_pass(1, HALF, HALF)
-        for b in range(2):
-            in_quarters(1, b, (GOT_V, GOT_V + 1024))
-            c_pass(2, HALF * b, HALF)
-            c_pass(3, HALF * b, HALF)
+        in_quarters(1, 0, (GOT_V + 512, GOT_V + 6912))
+        order_wc_scale(3, GOT_V + 1024)
+        c_pass(2, 0, HALF)
+        c_pass(3, 0, HALF)
+        in_quarters(1, 1, (GOT_V, GOT_V + 6912))
+        c_pass(2, HALF, HALF)
+        c_pass(3, HALF, HALF)
 
         rate_sb = kept([P, NT], F32, "rate_sb")
         wo_codes = placed([P, N], U32, "wo_codes", 0)

@@ -25,7 +25,7 @@ NT = N // P
 QUARTER = 256
 RUN = 2
 EARLY = 5
-WARM_UPS = 3
+WARM_UPS = 4
 GOT_V = 8192
 WD_AT = 18432
 ROWS_AT = WD_AT + 16384

from contextlib import ExitStack

import concourse.mybir as mybir

K, H, N, T, S = 2048, 512, 768, 2048, 1024
FLOPS = 2 * K * H * S * 2 + 2 * H * N * S

F32 = mybir.dt.float32
BF16 = mybir.dt.bfloat16
I32 = mybir.dt.int32
U32 = mybir.dt.uint32
U16 = mybir.dt.uint16
U8 = mybir.dt.uint8
FP8X4 = mybir.dt.float8_e4m3fn_x4
FP4X4 = mybir.dt.float4_e2m1fn_x4
ACT = mybir.ActivationFunctionType
MULT = mybir.AluOpType.mult

P = 128
PASSES = K // 512
HALF = 512
CHUNK = 128
PAIR = 256
NT = N // P
QUARTER = 256
RUN = 2
EARLY = 5
WARM_UPS = 4
GOT_V = 8192
WD_AT = 18432
ROWS_AT = WD_AT + 16384


def tile_list_momentum_block_steps_kernel(
    tc, tab, offs, wd, wc_words, wc_scales, wo_words, wo_scales, rate, out
):
    nc = tc.nc
    with ExitStack() as ctx:
        keep = ctx.enter_context(tc.tile_pool(name="keep", bufs=1))
        shared = ctx.enter_context(tc.tile_pool(name="shared", bufs=1))
        psum = ctx.enter_context(tc.psum_pool(name="psum", bufs=1))

        def placed(shape, dtype, name, offset):
            return shared.tile(shape, dtype, name=name, align_bytes=64, offset=offset)

        def kept(shape, dtype, name):
            return keep.tile(shape, dtype, name=name, align_bytes=64)

        def bank(shape, b):
            return psum.tile(shape, F32, name=f"bank{b}")

        def words(tile):
            return tile.rearrange("p a e -> p (a e)").bitcast(I32).rearrange("p (a e) -> p a e", a=tile.shape[1])

        offsets = keep.tile([P, S // 16], U16, name="offsets")
        tab_scale = placed([P, T], U8, "tab_scale", ROWS_AT)
        wcs_raw = kept([P, PASSES, H], U8, "wcs_raw")
        warm = keep.tile([P, 2], F32, name="warm")

        nc.vector.memset(warm[:, 0:1], 1.0)
        nc.scalar.activation(warm[:, 1:2], warm[:, 0:1], ACT.Abs_reciprocal_sqrt, bias=1.0)
        nc.vector.memset(wcs_raw[:].rearrange("p a e -> p (a e)").bitcast(I32), 0)
        for m in range(2):
            nc.vector.memset(tab_scale[64 * m + 32 : 64 * m + 64, :].bitcast(I32), 0)

        nc.sync.dma_start(offsets[:], offs)
        for m in range(2):
            nc.sync.dma_start(
                tab_scale[64 * m : 64 * m + 32, :].bitcast(I32),
                tab[m, 512 * T :].rearrange("(h q t) -> q h t", h=2, q=16).bitcast(I32),
            )
        for r in range(4):
            nc.scalar.dma_start(words(wcs_raw[r:P:32]), wc_scales.bitcast(I32)[:, r:16:4, :].rearrange("a q e -> q a e"))

        def load_tab(m, tile):
            nc.sync.dma_start(tile[:].bitcast(I32), tab[m, 0 : 512 * T].rearrange("(p w) -> p w", p=P).bitcast(I32))
            return tile

        def load_wc(m, raw):
            nc.sync.dma_start(words(raw[:]), wc_words.bitcast(I32)[2 * m : 2 * m + 2].rearrange("a p e -> p a e"))
            return raw

        tab_words = [load_tab(0, kept([P, T], U32, "tab_words0"))]
        wc_raw = [load_wc(m, placed([P, 2, H], U16, f"wc_raw{m}", ROWS_AT + 2048 * (m + 1))) for m in range(2)]

        got = kept([P, S], U8, "got")
        nc.vector.tensor_copy(got[:], tab_scale[:].indirect(offsets[:]))

        planes = []

        def move_rows(m, queues):
            planes.append(placed([P, 2, S], U8, f"planes{m}", ROWS_AT + 2048 * m))
            for q in (0, 2, 1, 3):
                queues[q // 2].dma_start(
                    words(planes[m][32 * q : 32 * q + 4]), got[64 * m + 8 * q : 64 * m + 8 * (q + 1), :].bitcast(I32)
                )

        move_rows(0, (nc.sync, nc.scalar))
        tab_words.append(load_tab(1, placed([P, T], U32, "tab_words1", 0)))
        wc_codes = [kept([P, H], U16, f"wc_codes{a}") for a in range(PASSES)]

        def order_wc(a):
            nc.scalar.copy(
                wc_codes[a][:].rearrange("p (t c i) -> p c t i", t=4, i=8),
                wc_raw[a // 2][:, a % 2, :].rearrange("p (c i t) -> p c t i", t=4, i=8),
            )

        for a in range(PASSES):
            order_wc(a)
        move_rows(1, (nc.sync, nc.sync))
        wd_rows = [wd[512 * a : 512 * (a + 1), :].rearrange("(p i) r -> p i r", i=4) for a in range(PASSES)]
        wd_raw = {(a, 0): kept([P, 4, H], F32, f"wd_raw{a}") for a in range(1, PASSES)}
        wd_raw[0, 0] = kept([P, 4, H // 2], F32, "wd_raw0_left")
        wd_raw[0, H // 2] = placed([P, 4, H // 2], F32, "wd_raw0_right", WD_AT + 6144)
        for r0 in (0, H // 2):
            nc.sync.dma_start(wd_raw[0, r0][:], wd_rows[0][:, :, r0 : r0 + H // 2])
        for a in range(1, PASSES):
            nc.sync.dma_start(wd_raw[a, 0][:], wd_rows[a])

        wc_planes = {}

        def order_wc_scale(a, offset):
            wc_planes[a] = placed([P, H], U8, f"wc_plane{a}", offset)
            nc.vector.tensor_copy(
                wc_planes[a][:].rearrange("p (t c i) -> p c t i", t=4, i=16),
                wcs_raw[:, a, :].rearrange("p (c i t) -> p c t i", t=4, i=16),
            )

        v_planes = [planes[a // 2][:, a % 2, :] for a in range(PASSES)]
        v_codes = [[kept([P, 2, HALF], U16, f"v_codes{m}{b}") for b in range(2)] for m in range(2)]

        def gather_words(m, c0, tile):
            width = tile.shape[1]
            nc.vector.tensor_copy(tile[:], tab_words[m][:].indirect(offsets[:, c0 // 16 : (c0 + width) // 16]))
            return m, c0, tile

        def part_words(m, c0, tile):
            b, o = divmod(c0, HALF)
            nc.vector.tensor_copy(
                v_codes[m][b][:, :, o : o + tile.shape[1]].rearrange("p h (c i) -> p c h i", i=8),
                tile[:].bitcast(U16).rearrange("p (c i h) -> p c h i", i=8, h=2),
            )

        def v_operand(a, c0, width):
            m, h = divmod(a, 2)
            b, o = divmod(c0, HALF)
            return v_codes[m][b][:, h, o : o + width].bitcast(FP4X4), v_planes[a][:, c0 : c0 + width]

        idle = bank([P, HALF], 7)
        wc_bytes = wcs_raw[:].rearrange("p a e -> p (a e)")
        for w in range(WARM_UPS):
            nc.tensor.matmul_mx(
                out=idle[:],
                lhsT=wc_bytes[:, 0 : 2 * P].bitcast(FP4X4),
                lhsT_scale=wc_bytes[:, 0:P],
                rhs=wc_bytes[:, 0 : 2 * HALF].bitcast(FP4X4),
                rhs_scale=wc_bytes[:, 0:HALF],
                start=True,
                stop=True,
            )
        c_acc = [[bank([P, HALF], 4 * b + t) for t in range(4)] for b in range(2)]

        def c_pass(a, c0, width):
            b, o = divmod(c0, HALF)
            rhs, rhs_scale = v_operand(a, c0, width)
            for t in range(4):
                nc.tensor.matmul_mx(
                    out=c_acc[b][t][:, o : o + width],
                    lhsT=wc_codes[a][:, P * t : P * (t + 1)].bitcast(FP4X4),
                    lhsT_scale=wc_planes[a][:, P * t : P * (t + 1)],
                    rhs=rhs,
                    rhs_scale=rhs_scale,
                    start=(a == 0 and o == 0),
                    stop=(a == PASSES - 1),
                )

        def in_quarters(m, b, at):
            pieces = [
                gather_words(m, HALF * b + QUARTER * e, placed([P, QUARTER], U32, f"got{m}{b}{e}", at[e])) for e in range(2)
            ]
            for piece in pieces:
                part_words(*piece)

        in_quarters(0, 0, (GOT_V + 2048, GOT_V + 5632))
        order_wc_scale(0, GOT_V + 2048)
        order_wc_scale(1, GOT_V + 2560)
        c_pass(0, 0, HALF)
        c_pass(1, 0, HALF)
        piece = gather_words(0, HALF, placed([P, HALF], U32, "got01", GOT_V + 3840))
        order_wc_scale(2, GOT_V + 5888)
        part_words(*piece)
        c_pass(0, HALF, HALF)
        c_pass(1, HALF, HALF)
        in_quarters(1, 0, (GOT_V + 512, GOT_V + 6912))
        order_wc_scale(3, GOT_V + 1024)
        c_pass(2, 0, HALF)
        c_pass(3, 0, HALF)
        in_quarters(1, 1, (GOT_V, GOT_V + 6912))
        c_pass(2, HALF, HALF)
        c_pass(3, HALF, HALF)

        rate_sb = kept([P, NT], F32, "rate_sb")
        wo_codes = placed([P, N], U32, "wo_codes", 0)
        nc.sync.dma_start(wo_codes[:].bitcast(I32), wo_words[0].rearrange("p e i -> p (e i)").bitcast(I32))
        wos = placed([P, N], U8, "wos", 4096)
        for r in range(4):
            nc.sync.dma_start(wos[r:P:32, :].bitcast(I32), wo_scales[0, r:16:4, :].bitcast(I32))
        with nc.allow_non_contiguous_dma(reason="one rate for each partition and row tile"):
            nc.sync.dma_start(rate_sb[:], rate.rearrange("(u p) -> p u", p=P))

        wd_bf = [[kept([P, 2, P, 4], BF16, f"wd_bf{a}{s}") for s in range(2)] for a in range(PASSES)]
        wd_codes = [kept([P, H], U32, f"wd_codes{a}") for a in range(PASSES)]
        wd_scale = [kept([P, H], U8, f"wd_scale{a}") for a in range(PASSES)]

        def cast_wd(a, r0, copy):
            raw = wd_raw[a, r0]
            for s in range(2):
                copy(
                    wd_bf[a][s][:, :, r0 // 4 : (r0 + raw.shape[2]) // 4, :].rearrange("p t m i -> p m i t"),
                    raw[:].rearrange("p i (m t) -> p m i t", t=4)[:, :, :, 2 * s : 2 * s + 2],
                )

        def quant_wd(a, s):
            nc.vector.quantize_mx(
                out=wd_codes[a][:, 2 * P * s : 2 * P * (s + 1)].bitcast(FP8X4),
                scales=wd_scale[a][:, 2 * P * s : 2 * P * (s + 1)],
                in_=wd_bf[a][s][:].rearrange("p t m i -> p (t m i)"),
            )

        sq = [placed([P, 4, HALF], F32, f"sq{b}", WD_AT + 8192 * b) for b in range(2)]
        damp = [kept([P, PAIR // RUN, 4, RUN], F32, f"damp{g}") for g in range(S // PAIR)]

        def squares(b):
            for t in range(4):
                nc.scalar.activation(sq[b][:, t, :], c_acc[b][t][:], ACT.Square)

        def rsqrt(g):
            b, o = divmod(PAIR * g, HALF)
            nc.scalar.activation(
                damp[g][:],
                sq[b][:, :, o : o + PAIR].rearrange("p t (c e) -> p c t e", e=RUN),
                ACT.Abs_reciprocal_sqrt,
                bias=1.0,
            )

        cast_wd(0, 0, nc.scalar.copy)
        cast_wd(0, H // 2, nc.scalar.copy)
        squares(0)
        squares(1)
        rsqrt(0)
        for a in range(PASSES):
            if a > 0:
                cast_wd(a, 0, nc.vector.tensor_copy)
            quant_wd(a, 0)
            quant_wd(a, 1)
        for g in range(1, 4):
            rsqrt(g)

        d_acc = {}

        def d_order(i):
            return list(range(PASSES)) if i < EARLY else list(reversed(range(PASSES)))

        def d_pass(a, i):
            if a == d_order(i)[0]:
                d_acc[i] = bank([P, 4, CHUNK], i)
            rhs, rhs_scale = v_operand(a, CHUNK * i, CHUNK)
            for t in range(4):
                nc.tensor.matmul_mx(
                    out=d_acc[i][:, t, :],
                    lhsT=wd_codes[a][:, P * t : P * (t + 1)].bitcast(FP8X4),
                    lhsT_scale=wd_scale[a][:, P * t : P * (t + 1)],
                    rhs=rhs,
                    rhs_scale=rhs_scale,
                    start=(a == d_order(i)[0] and t == 0),
                    stop=(a == d_order(i)[-1] and t == 3),
                )

        h_bf = [kept([P, 2, CHUNK, 4], BF16, f"h_bf{g}") for g in range(S // PAIR)]
        h_codes = [kept([P, PAIR], U32, f"h_codes{g}") for g in range(S // PAIR)]
        h_scale = [kept([P, PAIR], U8, f"h_scale{g}") for g in range(S // PAIR)]

        def damp_chunk(i):
            g, e = divmod(i, 2)
            runs = CHUNK // RUN
            nc.vector.tensor_tensor(
                h_bf[g][:, e].rearrange("p (c n) t -> p c t n", n=RUN),
                d_acc[i][:].rearrange("p t (c n) -> p c t n", n=RUN),
                damp[g][:, runs * e : runs * (e + 1)],
                MULT,
            )

        def quant_h(i, chunks):
            g, e = divmod(i, 2)
            nc.vector.quantize_mx(
                out=h_codes[g][:, CHUNK * e : CHUNK * (e + chunks)].bitcast(FP8X4),
                scales=h_scale[g][:, CHUNK * e : CHUNK * (e + chunks)],
                in_=h_bf[g][:, e : e + chunks].rearrange("p c n t -> p (c n t)"),
            )

        def y_cols(i, chunks, banks):
            g, e = divmod(i, 2)
            per_bank = NT // len(banks)
            cols = slice(CHUNK * e, CHUNK * (e + chunks))
            accs = [bank([P, per_bank, CHUNK * chunks], b) for b in banks]
            for u in range(NT):
                nc.tensor.matmul_mx(
                    out=accs[u // per_bank][:, u % per_bank, :],
                    lhsT=wo_codes[:, P * u : P * (u + 1)].bitcast(FP8X4),
                    lhsT_scale=wos[:, P * u : P * (u + 1)],
                    rhs=h_codes[g][:, cols].bitcast(FP8X4),
                    rhs_scale=h_scale[g][:, cols],
                    start=True,
                    stop=True,
                )
            return [(acc, per_bank * bk) for bk, acc in enumerate(accs)]

        made = {}

        def result(u0, rows, c0, width):
            made[(c0, u0)] = kept([P, rows, width], F32, f"res{c0}_{u0}")
            return made[(c0, u0)]

        def store(res, u0, c0):
            rows, width = res.shape[1], res.shape[2]
            nc.sync.dma_start(out[P * u0 : P * (u0 + rows), c0 : c0 + width].rearrange("(e p) j -> p e j", p=P), res[:])

        def on_vector(res, acc, u0):
            rates = rate_sb[:, u0 : u0 + acc.shape[1]].unsqueeze(2).to_broadcast(acc.shape)
            nc.vector.tensor_tensor(res, acc[:], rates, MULT)

        def on_scalar(res, acc, u0):
            for e in range(acc.shape[1]):
                nc.scalar.activation(res[:, e, :], acc[:, e, :], ACT.Copy, scale=rate_sb[:, u0 + e : u0 + e + 1])

        def empty(engine, part, c0):
            acc, u0 = part
            res = result(u0, acc.shape[1], c0, acc.shape[2])
            engine(res[:], acc, u0)
            store(res, u0, c0)

        def d_rest(i):
            for a in d_order(i)[2 if i < EARLY else 0 :]:
                d_pass(a, i)

        for a in (0, 1):
            for i in range(EARLY):
                d_pass(a, i)
        for i in range(4):
            d_pass(2, i)
        for i in range(2):
            d_pass(3, i)
        d_rest(4)
        for a in d_order(5)[:2]:
            d_pass(a, 5)
        for i in range(2, 4):
            d_pass(3, i)
        for a in d_order(5)[2:]:
            d_pass(a, 5)
        damp_chunk(0)
        damp_chunk(1)
        quant_h(0, 2)
        pair0 = y_cols(0, 2, (7, 0, 1))
        for e in range(2):
            empty(on_scalar, (pair0[0][0][:, e : e + 1, :], e), 0)
        for part in pair0[1:]:
            empty(on_scalar, part, 0)
        d_rest(6)
        for i in (2, 3, 4):
            damp_chunk(i)
        quant_h(2, 2)
        pair1 = y_cols(2, 2, (2, 3, 4))
        damp_chunk(5)
        damp_chunk(6)
        quant_h(4, 2)
        quant_h(6, 1)
        empty(on_scalar, pair1[0], PAIR)
        empty(on_scalar, pair1[1], PAIR)
        empty(on_vector, pair1[2], PAIR)
        d_rest(7)
        pair2 = y_cols(4, 2, (0, 1, 5))
        damp_chunk(7)
        quant_h(7, 1)
        empty(on_scalar, pair2[0], 2 * PAIR)
        empty(on_scalar, pair2[1], 2 * PAIR)
        empty(on_vector, pair2[2], 2 * PAIR)
        ends = [result(3 * k, 3, 3 * PAIR, PAIR) for k in range(2)]
        for e, banks in enumerate(((6, 2), (3, 4))):
            parts = y_cols(6 + e, 1, banks)
            for k, engine in enumerate((on_scalar, on_vector)):
                engine(ends[k][:, :, CHUNK * e : CHUNK * (e + 1)], *parts[k])
        for k in range(2):
            store(ends[k], 3 * k, 3 * PAIR)
